import numpy as np
import ml_dtypes


def mxq(x, axis, fmt="e4m3"):
    dtype, down = {"e4m3": (ml_dtypes.float8_e4m3fn, 7), "e5m2": (ml_dtypes.float8_e5m2, 14)}[fmt]
    v = np.moveaxis(np.asarray(x, np.float32).astype(ml_dtypes.bfloat16).astype(np.float64), axis, -1)
    blocks = v.reshape(v.shape[:-1] + (-1, 32))
    amax = np.abs(blocks).max(-1, keepdims=True)
    byte = np.maximum(np.where(amax > 0, np.frexp(amax)[1] - 1 + 127, 0) - down, 1)
    scale = np.exp2(byte - 127.0)
    codes = (blocks / scale).astype(np.float32).astype(dtype).astype(np.float64)
    return np.moveaxis((codes * scale).reshape(v.shape), -1, axis)


WIDE = False


def mx_kscale(k):
    if not WIDE:
        return np.ones(k)
    levels = np.array([10, -10, 5, -5, 0])
    if k % 512:
        return np.exp2(np.random.permutation(np.resize(levels, k // 32))).repeat(32)
    a = np.empty((k // 512, 16))
    for p in range(k // 512):
        a[p, :8] = np.random.permutation(np.resize(levels, 8))
        for g in range(8):
            far = levels[np.abs(levels - a[p, g]) >= 10]
            a[p, g + 8] = far[np.random.randint(len(far))]
    return np.exp2(a.ravel()).repeat(32)


def f64(x):
    return np.asarray(x).astype(np.float64)


def striped(idx):
    return np.tile(idx.reshape(-1, 16).T, (8, 1)).astype(np.uint16)


def unstriped(offs):
    return offs[:16].T.reshape(-1).astype(np.int64)


E2M1 = np.array([0.0, 0.5, 1.0, 1.5, 2.0, 3.0, 4.0, 6.0, -0.0, -0.5, -1.0, -1.5, -2.0, -3.0, -4.0, -6.0])


def pack_weight(w, fmt):
    k, n = w.shape
    w = f64(np.asarray(w, np.float32).astype(ml_dtypes.bfloat16)).reshape(k // 32, 32, n)
    amax = np.abs(w).max(1)
    if fmt == "e4m3":
        byte = np.frexp(amax)[1] - 1 + 127 - 7
    else:
        mant, ex = np.frexp(amax / 6.0)
        byte = np.where(mant > 0.5, ex, ex - 1) + 127
    byte = np.clip(np.where(amax > 0, byte, 1), 1, 254)
    scaled = (w * np.exp2(127.0 - byte)[:, None, :]).reshape(k, n).astype(np.float32)
    by_word = np.ascontiguousarray(scaled.reshape(k // 512, 128, 4, n).transpose(0, 1, 3, 2))
    if fmt == "e4m3":
        words = by_word.astype(ml_dtypes.float8_e4m3fn).view(np.uint8)
    else:
        c = by_word.astype(ml_dtypes.float4_e2m1fn).view(np.uint8) & 0xF
        words = (c[..., 0::2] | (c[..., 1::2] << 4)).reshape(k // 512, 128, 2 * n)
    return np.ascontiguousarray(words), np.ascontiguousarray(byte.astype(np.uint8).reshape(k // 512, 16, n))


def unpack_weight(words, scales, fmt):
    g, _, n = scales.shape
    words = np.ascontiguousarray(words).reshape(g, 128, n, -1)
    if fmt == "e4m3":
        vals = words.view(ml_dtypes.float8_e4m3fn).astype(np.float64)
    else:
        nib = np.empty((g, 128, n, 4), np.uint8)
        nib[..., 0::2] = words & 0xF
        nib[..., 1::2] = words >> 4
        vals = E2M1[nib]
    vals = vals * np.repeat(np.exp2(scales.astype(np.float64) - 127.0), 8, axis=1)[..., None]
    return vals.transpose(0, 1, 3, 2).reshape(g * 512, n)


def gelu(v):
    return 0.5 * v * (1.0 + np.tanh(np.sqrt(2.0 / np.pi) * (v + 0.044715 * v**3)))


def bf(x):
    return np.asarray(x, np.float32).astype(ml_dtypes.bfloat16)


def planes(Y):
    n, m = Y.shape
    b = f64(bf(Y)).reshape(n // 32, 32, m)
    amax = np.abs(b).max(1)
    byte = np.clip(np.where(amax > 0, np.frexp(amax)[1] - 1 + 127 - 7, 1), 1, 254)
    codes = (b * np.exp2(127.0 - byte)[:, None, :]).reshape(n, m).astype(np.float32).astype(ml_dtypes.float8_e4m3fn).view(np.uint8)
    words = codes.reshape(n // 512, 128, 4, m).transpose(0, 1, 3, 2)
    return np.ascontiguousarray(words), np.ascontiguousarray(byte.astype(np.uint8).reshape(n // 512, 16, m))


K, M, H, N, T, TF, S, T2, P = 1024, 512, 1024, 512, 2048, 1024, 512, 2048, 1024

def setup_inputs():
    n = np.random.standard_normal
    s, s2, u = mx_kscale(K)[:, None], mx_kscale(M)[:, None], mx_kscale(H)[:, None]
    perm = np.random.permutation(T2)
    d = {}
    d["tab_words"], d["tab_scales"] = pack_weight(n((K, T)) * s, "e4m3")
    d["tab2_words"], d["tab2_scales"] = pack_weight(n((M, TF)) * s2, "e4m3")
    d["offs"] = striped(np.random.permutation(T)[:S])
    d["offs2"] = striped(np.random.permutation(TF)[:S])
    d["offs3"] = striped(perm[:S])
    d["offs4"] = striped(perm[S:2 * S])
    d["offs5"] = striped(np.random.permutation(T2)[:P])
    d["wi"] = (2.0 * n((K, H)) / K**0.5 / s).astype(np.float32)
    d["wf_words"], d["wf_scales"] = pack_weight(n((M, H)) / M**0.5 / s2, "e2m1")
    d["sp"] = n((H, S)).astype(np.float32)
    d["wg1"] = (0.18 * np.exp(0.3 * np.clip(n((128, S)), -1.2, 1.2))).astype(np.float32)
    d["wg2"] = (0.27 * np.exp(0.3 * np.clip(n((128, S)), -1.2, 1.2))).astype(np.float32)
    d["page0"] = np.random.uniform(-1.7, 1.7, (H, T2)).astype(np.float32)
    d["gain"] = (np.random.uniform(0.6, 1.4, H) * u[:, 0]).astype(np.float32)
    d["wt"] = (n((H, N)) / H**0.5 / u).astype(np.float32)
    d["wb_words"], d["wb_scales"] = pack_weight(0.6 * n((H, N)) * np.exp(0.8 * n(N)) / H**0.5 / u, "e4m3")
    return d

def reference(tab_words, tab_scales, tab2_words, tab2_scales, offs, offs2, offs3, offs4, offs5, wi, wf_words, wf_scales, sp, wg1, wg2, page0, gain, wt, wb_words, wb_scales):
    v = unpack_weight(tab_words, tab_scales, "e4m3")[:, unstriped(offs)]
    v2 = unpack_weight(tab2_words, tab2_scales, "e4m3")[:, unstriped(offs2)]
    a = mxq(f64(wi), 0, "e4m3").T @ v
    h1 = a + np.tanh(a)
    f = unpack_weight(wf_words, wf_scales, "e2m1").T @ v2
    h2 = np.abs(f - f64(sp))
    page = f64(page0).copy()
    page[:, unstriped(offs3)] = np.tile(f64(wg1), (H // 128, 1)) * h1
    page[:, unstriped(offs4)] = np.tile(f64(wg2), (H // 128, 1)) * h2
    x = page[:, unstriped(offs5)]
    z = mxq((x + np.sin(x)) * f64(gain)[:, None], 0, "e4m3")
    e = mxq(f64(wt), 0, "e4m3").T @ z
    b = unpack_weight(wb_words, wb_scales, "e4m3").T @ z
    y = np.tanh(e) + b
    words, scales = planes(y)
    return y, words, scales

@@ -1,0 +1,403 @@
+from contextlib import ExitStack
+
+import concourse.mybir as mybir
+from concourse.masks import make_identity
+
+K, M, H, N, T, TF, S, T2, PJ = 1024, 512, 1024, 512, 2048, 1024, 512, 2048, 1024
+FLOPS = 2 * (K * H * S + M * H * S + 2 * H * N * PJ)
+
+F32 = mybir.dt.float32
+BF16 = mybir.dt.bfloat16
+I32 = mybir.dt.int32
+U32 = mybir.dt.uint32
+U16 = mybir.dt.uint16
+U8 = mybir.dt.uint8
+FP8X4 = mybir.dt.float8_e4m3fn_x4
+FP4X4 = mybir.dt.float4_e2m1fn_x4
+ACT = mybir.ActivationFunctionType
+ALU = mybir.AluOpType
+
+P = 128
+PACK = 4
+PASS = P * PACK
+CH = 256
+ON_PE = 4
+
+
+def tile_list_blade_edge_register_kernel(
+    tc, tab_words, tab_scales, tab2_words, tab2_scales, offs, offs2, offs3, offs4, offs5,
+    wi, wf_words, wf_scales, sp, wg1, wg2, page0, gain, wt, wb_words, wb_scales,
+    out_0, out_1, out_2,
+):
+    nc = tc.nc
+    with ExitStack() as ctx:
+        keep = ctx.enter_context(tc.tile_pool(name="keep", bufs=1))
+        ring = ctx.enter_context(tc.tile_pool(name="ring", bufs=2))
+        psum = ctx.enter_context(tc.psum_pool(name="psum", bufs=3))
+
+        def load_list(src, name):
+            lst = keep.tile(list(src.shape), U16, name=name)
+            nc.sync.dma_start(lst[:], src)
+            return lst
+
+        def scale_plane(width, name):
+            plane = keep.tile([P, width], U8, name=name, align_bytes=64)
+            nc.vector.memset(plane[:].bitcast(I32), 0)
+            return plane
+
+        def load_scales(queue, plane, scales):
+            passes = scales.shape[0]
+            for q in range(4):
+                queue.dma_start(
+                    out=plane[32 * q : 32 * q + 4 * passes, :].bitcast(I32),
+                    in_=scales[:, 4 * q : 4 * q + 4, :].bitcast(I32),
+                )
+
+        def load_words(words, a, name, tag):
+            width = words.shape[2]
+            tile = keep.tile([P, width], U32, name=name, tag=tag, align_bytes=64)
+            nc.sync.dma_start(out=tile[:].bitcast(I32), in_=words[a].rearrange("p n t -> p (n t)").bitcast(I32))
+            return tile
+
+        def gather(src, lst, dtype, name):
+            got = keep.tile([P, S], dtype, name=name, align_bytes=64)
+            nc.vector.tensor_copy(got[:], src[:].indirect(lst[:]))
+            return got
+
+        def dealt_rows(mat, a, t):
+            return mat[PASS * a : PASS * (a + 1), :].rearrange("(p t) c -> p t c", t=PACK)[:, t, :]
+
+        tab2_plane = scale_plane(TF, "tab2_plane")
+        wf_plane = scale_plane(H, "wf_plane")
+        zero_in = keep.tile([P, 1], F32, name="zero_in")
+        nc.vector.memset(zero_in[:], 0.0)
+        zero = keep.tile([P, 1], F32, name="zero")
+        nc.scalar.activation(zero[:], zero_in[:], ACT.Silu)
+        tab_plane = scale_plane(T, "tab_plane")
+        wb_plane_raw = scale_plane(N, "wb_plane_raw")
+
+        pages = {}
+        setpoints = {}
+
+        def load_page(k):
+            pages[k] = keep.tile([P, T2], F32, name="page%d" % k)
+            nc.sync.dma_start(out=pages[k][:], in_=dealt_rows(page0, k // 4, k % 4))
+
+        def load_sp(k):
+            setpoints[k] = ring.tile([P, S], F32, name="sp%d" % k, tag="sp", bufs=8, align_bytes=64)
+            nc.sync.dma_start(out=setpoints[k][:], in_=dealt_rows(sp, k // 4, k % 4))
+
+        def load_wg(wg, name):
+            tile = keep.tile([P, PACK, S], F32, name=name)
+            for q in range(4):
+                nc.sync.dma_start(out=tile[32 * q : 32 * q + 32, :, :], in_=wg.rearrange("(p t) j -> p t j", t=PACK))
+            return tile
+
+        def load_raw(w, a, cols, name):
+            raw = ring.tile([P, PACK, PASS], F32, name=name, tag="raw")
+            nc.sync.dma_start(out=raw[:], in_=w[PASS * a : PASS * (a + 1), cols].rearrange("(p i) c -> p i c", i=PACK))
+            return raw
+
+        def quantise(grouped, name):
+            width = grouped.shape[1] // PACK
+            codes = keep.tile([P, width], U32, name=name + "_codes", align_bytes=64)
+            plane = keep.tile([P, width], U8, name=name + "_plane", align_bytes=64)
+            nc.vector.quantize_mx(out=codes[:].bitcast(FP8X4), scales=plane[:], in_=grouped)
+            return codes, plane
+
+        def bf_tile(width, name):
+            return ring.tile([P, width], BF16, name=name, tag="bf", bufs=3, align_bytes=64)
+
+        l2 = load_list(offs2, "l2")
+        l4 = load_list(offs4, "l4")
+        load_scales(nc.sync, tab2_plane, tab2_scales)
+        tab2_w = load_words(tab2_words, 0, "tab2_w", "tab2_w")
+        wf_w = {}
+
+        def load_wf(a):
+            wf_w[a] = keep.tile([P, 2 * PASS], U8, name="wf_w%d" % a, align_bytes=64)
+            nc.sync.dma_start(out=wf_w[a][:].bitcast(I32), in_=wf_words[0, :, 2 * PASS * a : 2 * PASS * (a + 1)].bitcast(I32))
+
+        load_wf(0)
+        ident = keep.tile([P, P], F32, name="ident")
+        make_identity(nc, ident[:])
+        load_scales(nc.gpsimd, wf_plane, wf_scales)
+        load_sp(0)
+        wg2_t = load_wg(wg2, "wg2_t")
+        load_page(0)
+
+        v2 = gather(tab2_w, l2, U32, "v2")
+        v2_plane = gather(tab2_plane, l2, U8, "v2_plane")
+
+        def add_transposed(bank, cols, first, second):
+            nc.tensor.matmul(bank[:, cols], first, ident[:], start=True, stop=False, is_transpose=True)
+            nc.tensor.matmul(bank[:, cols], second, ident[:], start=False, stop=True, is_transpose=True)
+
+        f_t = {}
+
+        def product_f(a):
+            f_t[a] = keep.tile([P, PACK, 4, P], F32, name="f_t%d" % a, tag="at%d" % a)
+            for jb in range(4):
+                jc = slice(P * jb, P * (jb + 1))
+                bank = psum.tile([P, PASS], F32, name="f_bank", tag="mx")
+                nc.tensor.matmul_mx(
+                    out=bank[:], lhsT=v2[:, jc].bitcast(FP8X4), lhsT_scale=v2_plane[:, jc],
+                    rhs=wf_w[a][:].bitcast(FP4X4),
+                    rhs_scale=wf_plane[:, PASS * a : PASS * (a + 1)], start=True, stop=True,
+                )
+                dealt = bank[:].rearrange("j (m t) -> j t m", t=PACK)
+                if a == 0 and jb % 2 == 1:
+                    nc.vector.tensor_copy(f_t[a][:, :, jb, :], dealt)
+                else:
+                    nc.scalar.copy(f_t[a][:, :, jb, :], dealt)
+
+        def put_h2(k):
+            a, t = divmod(k, 4)
+            sp_bank = psum.tile([P, S], F32, name="sp_bank", tag="sp", bufs=2)
+            for jb in range(4):
+                jc = slice(P * jb, P * (jb + 1))
+                nc.tensor.transpose(sp_bank[:, jc], setpoints[k][:, jc], ident[:])
+            neg_sp = setpoints[k]
+            nc.scalar.activation(neg_sp[:], sp_bank[:], ACT.Copy, scale=-1.0)
+            bank = psum.tile([P, S], F32, name="h2_bank", tag="h")
+            for jb in range(4):
+                jc = slice(P * jb, P * (jb + 1))
+                add_transposed(bank, jc, f_t[a][:, t, jb, :], neg_sp[:, jc])
+            h2 = setpoints[k]
+            nc.scalar.activation(h2[:], bank[:], ACT.Abs, bias=zero[:])
+            nc.vector.tensor_tensor(pages[k][:].indirect(l4[:]), h2[:], wg2_t[:, t, :], ALU.mult)
+
+        wi_q = {}
+
+        def quantise_wi(raw, c, a):
+            grouped = bf_tile(PASS * PACK, "wi_bf")
+            nc.scalar.copy(
+                grouped[:].rearrange("p (c e i) -> p c i e", e=4, i=PACK),
+                raw[:].rearrange("p i (c e) -> p c i e", e=4),
+            )
+            wi_q[c, a] = quantise(grouped[:], "wi%d%d" % (c, a))
+
+        a_t = {}
+
+        def product_a(a):
+            a_t[a] = keep.tile([P, PACK, 2, 4, P], F32, name="a_t%d" % a, tag="at%d" % a)
+            for jb in range(4):
+                jc = slice(P * jb, P * (jb + 1))
+                bank = psum.tile([P, PASS], F32, name="a_bank", tag="mx")
+                for c in range(2):
+                    nc.tensor.matmul_mx(
+                        out=bank[:], lhsT=v[c][:, jc].bitcast(FP8X4), lhsT_scale=v_plane[4 * c : P, jc],
+                        rhs=wi_q[c, a][0][:].bitcast(FP8X4), rhs_scale=wi_q[c, a][1][:],
+                        start=(c == 0), stop=(c == 1),
+                    )
+                dealt = bank[:].rearrange("j (m t) -> j t m", t=PACK)
+                nc.scalar.activation(a_t[a][:, :, 0, jb, :], dealt, ACT.Tanh, bias=zero[:])
+                nc.scalar.copy(a_t[a][:, :, 1, jb, :], dealt)
+
+        def put_h1(k):
+            a, t = divmod(k, 4)
+            bank = psum.tile([P, S], F32, name="h1_bank", tag="h")
+            for jb in range(4):
+                add_transposed(bank, slice(P * jb, P * (jb + 1)), a_t[a][:, t, 0, jb, :], a_t[a][:, t, 1, jb, :])
+            h1 = a_t[a][:, t, 0, :, :].rearrange("p b m -> p (b m)")
+            nc.scalar.copy(h1, bank[:])
+            nc.vector.tensor_tensor(pages[k][:].indirect(l3[:]), h1, wg1_t[:, t, :], ALU.mult)
+
+        z_rows = {}
+        x_t = {}
+        s_t = {}
+
+        def fetch(k, j0, j1):
+            if j0 == 0:
+                x_t[k] = a_t[k // 4][:, k % 4, :, :, :].rearrange("p h b m -> p (h b m)")
+                if k % 2 == 0:
+                    s_t[k, 2] = ring.tile([P, 2, PJ], F32, name="s_pair", tag="raw")
+                s_t[k] = s_t[k - k % 2, 2][:, k % 2, :]
+            nc.vector.tensor_copy(x_t[k][:, j0:j1], pages[k][:].indirect(l5[:, j0 // 16 : j1 // 16]))
+            nc.scalar.activation(s_t[k][:, j0:j1], x_t[k][:, j0:j1], ACT.Sin, bias=zero[:])
+
+        def make_z_rows(k, j0, j1):
+            a, t = divmod(k, 4)
+            if a not in z_rows:
+                z_rows[a] = keep.tile([P, PACK, PJ], BF16, name="z_rows%d" % a, tag="tab_w%d" % a, align_bytes=64)
+            if k >= ON_PE:
+                nc.vector.tensor_tensor(s_t[k][:, j0:j1], x_t[k][:, j0:j1], s_t[k][:, j0:j1], ALU.add)
+                nc.scalar.activation(z_rows[a][:, t, j0:j1], s_t[k][:, j0:j1], ACT.Copy, scale=gain_t[:, a, t : t + 1])
+                return
+            for h0 in range(j0, j1, PASS):
+                sum_bank = psum.tile([P, PASS], F32, name="sum_bank", tag="sp", bufs=2)
+                for jb in range(4):
+                    jc = slice(h0 + P * jb, h0 + P * (jb + 1))
+                    add_transposed(sum_bank, slice(P * jb, P * (jb + 1)), x_t[k][:, jc], s_t[k][:, jc])
+                nc.scalar.copy(x_t[k][:, h0 : h0 + PASS], sum_bank[:])
+                back_bank = psum.tile([P, PASS], F32, name="back_bank", tag="h")
+                for jb in range(4):
+                    jc = slice(h0 + P * jb, h0 + P * (jb + 1))
+                    nc.tensor.transpose(back_bank[:, P * jb : P * (jb + 1)], x_t[k][:, jc], ident[:])
+                nc.scalar.activation(z_rows[a][:, t, h0 : h0 + PASS], back_bank[:], ACT.Copy, scale=gain_t[:, a, t : t + 1])
+
+        z_q = {}
+
+        def quantise_z(a, j0, j1):
+            grouped = bf_tile((j1 - j0) * PACK, "z_bf")
+            nc.scalar.copy(
+                grouped[:].rearrange("p (c e t) -> p c t e", e=4, t=PACK),
+                z_rows[a][:, :, j0:j1].rearrange("p t (c e) -> p c t e", e=4),
+            )
+            codes, plane = quantise(grouped[:], "z%d_%d" % (a, j0))
+            for j in range(j0, j1, CH):
+                z_q[a, j] = (codes[:, j - j0 : j - j0 + CH], plane[:, j - j0 : j - j0 + CH])
+
+        product_f(0)
+        put_h2(0)
+
+        load_sp(1)
+        load_page(1)
+        l1 = load_list(offs, "l1")
+        load_scales(nc.sync, tab_plane, tab_scales)
+        tab_w = [load_words(tab_words, c, "tab_w%d" % c, "tab_w%d" % c) for c in range(2)]
+        put_h2(1)
+        v_plane = gather(tab_plane, l1, U8, "v_plane")
+        v = [gather(tab_w[c], l1, U32, "v%d" % c) for c in range(2)]
+        load_sp(2)
+        load_wf(1)
+        raws = [load_raw(wi, c, slice(0, PASS), "wi_raw") for c in range(2)]
+        load_sp(3)
+        load_page(2)
+        load_sp(4)
+        load_page(3)
+        l3 = load_list(offs3, "l3")
+        wg1_t = load_wg(wg1, "wg1_t")
+        load_page(4)
+        put_h2(2)
+        quantise_wi(raws[0], 0, 0)
+        quantise_wi(raws[1], 1, 0)
+        put_h2(3)
+        product_f(1)
+        put_h2(4)
+        product_a(0)
+        l5 = load_list(offs5, "l5")
+        gain_t = keep.tile([P, 2, PACK], F32, name="gain_t")
+        nc.sync.dma_start(out=gain_t[:], in_=gain.rearrange("(a p t) -> p a t", a=2, t=PACK))
+        raws = [load_raw(wi, c, slice(PASS, 2 * PASS), "wi_raw") for c in range(2)]
+        for k in range(5, 8):
+            load_sp(k)
+        load_page(5)
+        wt_raws = [load_raw(wt, a, slice(0, N), "wt_raw") for a in range(2)]
+        load_page(6)
+        load_page(7)
+        wb_raw = ring.tile([P, 2, N], I32, name="wb_raw", tag="bf", bufs=3, align_bytes=64)
+        nc.sync.dma_start(out=wb_raw[:], in_=wb_words.rearrange("a p n t -> p a (n t)").bitcast(I32))
+        load_scales(nc.sync, wb_plane_raw, wb_scales)
+        put_h1(0)
+        put_h1(1)
+        quantise_wi(raws[0], 0, 1)
+        quantise_wi(raws[1], 1, 1)
+        put_h1(2)
+        put_h1(3)
+        for k in range(5, 8):
+            put_h2(k)
+        product_a(1)
+        for k in range(4, 8):
+            put_h1(k)
+        wt_q = []
+        for a in range(2):
+            grouped = bf_tile(N * PACK, "wt_bf")
+            nc.scalar.copy(
+                grouped[:].rearrange("p (t m i) -> p m i t", t=PACK, i=PACK),
+                wt_raws[a][:].rearrange("p i (m t) -> p m i t", t=PACK),
+            )
+            wt_q.append(quantise(grouped[:], "wt%d" % a))
+        wb_w = keep.tile([P, 2, N], U32, name="wb_w", tag="tab2_w", align_bytes=64)
+        wb_plane = keep.tile([P, N], U8, name="wb_plane", align_bytes=64)
+        nc.vector.tensor_copy(
+            wb_w[:].bitcast(I32).rearrange("p a (t m) -> p a m t", t=PACK),
+            wb_raw[:].rearrange("p a (m t) -> p a m t", t=PACK),
+        )
+        nc.vector.tensor_copy(
+            wb_plane[:].rearrange("p (t m) -> p t m", t=PACK),
+            wb_plane_raw[:].rearrange("p (m t) -> p t m", t=PACK),
+        )
+        for k in range(4):
+            fetch(k, 0, PJ)
+            if k % 2 == 1:
+                make_z_rows(k - 1, 0, PJ)
+                make_z_rows(k, 0, PJ)
+        quantise_z(0, 0, PJ // 2)
+        quantise_z(0, PJ // 2, PJ)
+
+        y_all = keep.tile([P, PACK, PJ], F32, name="y_all", tag="at0")
+        y_plane = keep.tile([P, PJ], U8, name="y_plane", align_bytes=64)
+        y_rows = out_0.rearrange("(p t) j -> p t j", t=PACK)
+        y_words = out_1[0].rearrange("p m t -> p (m t)").bitcast(I32)
+
+        def second_stage(j0):
+            y = y_all[:, :, j0 : j0 + CH]
+            for u in range(2):
+                if u == 0:
+                    e_bank = psum.tile([P, 2, CH], F32, name="e_bank", tag="mx")
+                else:
+                    e_bank = psum.tile([P, 2, CH], F32, name="e_bank", tag="sp", bufs=2)
+                b_bank = psum.tile([P, 2, CH], F32, name="b_bank", tag="h")
+                for e in range(2):
+                    nc_cols = slice(P * (2 * u + e), P * (2 * u + e + 1))
+                    for a in range(2):
+                        nc.tensor.matmul_mx(
+                            out=e_bank[:, e, :], lhsT=wt_q[a][0][:, nc_cols].bitcast(FP8X4), lhsT_scale=wt_q[a][1][:, nc_cols],
+                            rhs=z_q[a, j0][0].bitcast(FP8X4), rhs_scale=z_q[a, j0][1], start=(a == 0), stop=(a == 1),
+                        )
+                for e in range(2):
+                    nc_cols = slice(P * (2 * u + e), P * (2 * u + e + 1))
+                    for a in range(2):
+                        nc.tensor.matmul_mx(
+                            out=b_bank[:, e, :], lhsT=wb_w[:, a, nc_cols].bitcast(FP8X4), lhsT_scale=wb_plane[4 * a : P, nc_cols],
+                            rhs=z_q[a, j0][0].bitcast(FP8X4), rhs_scale=z_q[a, j0][1], start=(a == 0), stop=(a == 1),
+                        )
+                tanh_e = ring.tile([P, 2, CH], F32, name="tanh_e", tag="sp", bufs=8, align_bytes=64)
+                nc.scalar.activation(tanh_e[:], e_bank[:], ACT.Tanh, bias=zero[:])
+                nc.vector.tensor_tensor(y[:, 2 * u : 2 * u + 2, :], b_bank[:], tanh_e[:], ALU.add)
+            nc.sync.dma_start(out=y_rows[:, :, j0 : j0 + CH], in_=y)
+            y_bf = ring.tile([P, CH * PACK], BF16, name="y_bf", tag="sp", bufs=8, align_bytes=64)
+            nc.vector.tensor_copy(
+                y_bf[:].rearrange("p (c e t) -> p c t e", e=4, t=PACK),
+                y.rearrange("p t (c e) -> p c t e", e=4),
+            )
+            y_codes = keep.tile([P, CH], U32, name="y_codes%d" % j0, align_bytes=64)
+            nc.vector.quantize_mx(out=y_codes[:].bitcast(FP8X4), scales=y_plane[:, j0 : j0 + CH], in_=y_bf[:])
+            nc.sync.dma_start(out=y_words[:, j0 : j0 + CH], in_=y_codes[:].bitcast(I32))
+
+        x_all = a_t[1][:].rearrange("p t h b m -> p t (h b m)")
+        z_rows[1] = keep.tile([P, PACK, PJ], BF16, name="z_rows1", tag="tab_w1", align_bytes=64)
+
+        s_early = keep.tile([P, 2, PACK, CH], F32, name="s_early", tag="tab_w0", align_bytes=64)
+        s_late = ring.tile([P, 2, PACK, CH], F32, name="s_late", tag="raw")
+
+        def chunk_tiles(n):
+            x0 = CH * (n % 2)
+            return x_all[:, :, x0 : x0 + CH], (s_early if n < 2 else s_late)[:, n % 2, :, :]
+
+        def fetch_chunk(n):
+            x, s = chunk_tiles(n)
+            for t in range(PACK):
+                nc.vector.tensor_copy(x[:, t, :], pages[4 + t][:].indirect(l5[:, n * CH // 16 : (n + 1) * CH // 16]))
+            nc.scalar.activation(s, x, ACT.Sin, bias=zero[:])
+
+        fetch_chunk(0)
+        fetch_chunk(1)
+        chunks = list(range(0, PJ, CH))
+        for n, j0 in enumerate(chunks):
+            jc = slice(j0, j0 + CH)
+            x, s = chunk_tiles(n)
+            nc.vector.tensor_tensor(s, x, s, ALU.add)
+            for t in range(PACK):
+                nc.scalar.activation(z_rows[1][:, t, jc], s[:, t, :], ACT.Copy, scale=gain_t[:, 1, t : t + 1])
+            if n + 2 < len(chunks):
+                fetch_chunk(n + 2)
+            quantise_z(1, j0, j0 + CH)
+            if n >= 1:
+                second_stage(chunks[n - 1])
+        second_stage(chunks[-1])
+        for q in range(4):
+            nc.sync.dma_start(
+                out=out_2[0, 4 * q : 4 * q + 4, :].bitcast(I32), in_=y_plane[32 * q : 32 * q + 4, :].bitcast(I32)
+            )

@@ -94,7 +94,7 @@ def tile_list_blade_edge_register_kernel(
             return tile
 
         def load_raw(w, a, cols, name):
-            raw = ring.tile([P, PACK, PASS], F32, name=name, tag="raw")
+            raw = ring.tile([P, PACK, PASS], F32, name=name, tag="raw", bufs=3, align_bytes=64)
             nc.sync.dma_start(out=raw[:], in_=w[PASS * a : PASS * (a + 1), cols].rearrange("(p i) c -> p i c", i=PACK))
             return raw
 
@@ -121,7 +121,7 @@ def tile_list_blade_edge_register_kernel(
         load_wf(0)
         ident = keep.tile([P, P], F32, name="ident")
         make_identity(nc, ident[:])
-        load_scales(nc.gpsimd, wf_plane, wf_scales)
+        load_scales(nc.sync, wf_plane, wf_scales)
         load_sp(0)
         wg2_t = load_wg(wg2, "wg2_t")
         load_page(0)
@@ -169,12 +169,15 @@ def tile_list_blade_edge_register_kernel(
 
         wi_q = {}
 
-        def quantise_wi(raw, c, a):
+        def quantise_wi(raw, c, a, on_vector):
             grouped = bf_tile(PASS * PACK, "wi_bf")
-            nc.scalar.copy(
-                grouped[:].rearrange("p (c e i) -> p c i e", e=4, i=PACK),
-                raw[:].rearrange("p i (c e) -> p c i e", e=4),
-            )
+            dst = grouped[:].rearrange("p (c e i) -> p c i e", e=4, i=PACK)
+            src = raw[:].rearrange("p i (c e) -> p c i e", e=4)
+            split = on_vector // 4
+            if split > 0:
+                nc.vector.tensor_copy(dst[:, :split, :, :], src[:, :split, :, :])
+            if split < P:
+                nc.scalar.copy(dst[:, split:, :, :], src[:, split:, :, :])
             wi_q[c, a] = quantise(grouped[:], "wi%d%d" % (c, a))
 
         a_t = {}
@@ -183,7 +186,7 @@ def tile_list_blade_edge_register_kernel(
             a_t[a] = keep.tile([P, PACK, 2, 4, P], F32, name="a_t%d" % a, tag="at%d" % a)
             for jb in range(4):
                 jc = slice(P * jb, P * (jb + 1))
-                bank = psum.tile([P, PASS], F32, name="a_bank", tag="mx")
+                bank = psum.tile([P, PASS], F32, name="a_bank", tag=("mx", "h")[a])
                 for c in range(2):
                     nc.tensor.matmul_mx(
                         out=bank[:], lhsT=v[c][:, jc].bitcast(FP8X4), lhsT_scale=v_plane[4 * c : P, jc],
@@ -211,7 +214,7 @@ def tile_list_blade_edge_register_kernel(
             if j0 == 0:
                 x_t[k] = a_t[k // 4][:, k % 4, :, :, :].rearrange("p h b m -> p (h b m)")
                 if k % 2 == 0:
-                    s_t[k, 2] = ring.tile([P, 2, PJ], F32, name="s_pair", tag="raw")
+                    s_t[k, 2] = ring.tile([P, 2, PJ], F32, name="s_pair", tag="raw", bufs=3, align_bytes=64)
                 s_t[k] = s_t[k - k % 2, 2][:, k % 2, :]
             nc.vector.tensor_copy(x_t[k][:, j0:j1], pages[k][:].indirect(l5[:, j0 // 16 : j1 // 16]))
             nc.scalar.activation(s_t[k][:, j0:j1], x_t[k][:, j0:j1], ACT.Sin, bias=zero[:])
@@ -238,11 +241,12 @@ def tile_list_blade_edge_register_kernel(
 
         z_q = {}
 
-        def quantise_z(a, j0, j1):
+        def quantise_z(a, rows, j0):
+            j1 = j0 + rows.shape[2]
             grouped = bf_tile((j1 - j0) * PACK, "z_bf")
             nc.scalar.copy(
                 grouped[:].rearrange("p (c e t) -> p c t e", e=4, t=PACK),
-                z_rows[a][:, :, j0:j1].rearrange("p t (c e) -> p c t e", e=4),
+                rows.rearrange("p t (c e) -> p c t e", e=4),
             )
             codes, plane = quantise(grouped[:], "z%d_%d" % (a, j0))
             for j in range(j0, j1, CH):
@@ -254,7 +258,7 @@ def tile_list_blade_edge_register_kernel(
         load_sp(1)
         load_page(1)
         l1 = load_list(offs, "l1")
-        load_scales(nc.sync, tab_plane, tab_scales)
+        load_scales(nc.gpsimd, tab_plane, tab_scales)
         tab_w = [load_words(tab_words, c, "tab_w%d" % c, "tab_w%d" % c) for c in range(2)]
         put_h2(1)
         v_plane = gather(tab_plane, l1, U8, "v_plane")
@@ -270,8 +274,8 @@ def tile_list_blade_edge_register_kernel(
         wg1_t = load_wg(wg1, "wg1_t")
         load_page(4)
         put_h2(2)
-        quantise_wi(raws[0], 0, 0)
-        quantise_wi(raws[1], 1, 0)
+        quantise_wi(raws[0], 0, 0, PASS)
+        quantise_wi(raws[1], 1, 0, PASS // 2)
         put_h2(3)
         product_f(1)
         put_h2(4)
@@ -282,21 +286,21 @@ def tile_list_blade_edge_register_kernel(
         raws = [load_raw(wi, c, slice(PASS, 2 * PASS), "wi_raw") for c in range(2)]
         for k in range(5, 8):
             load_sp(k)
-        load_page(5)
         wt_raws = [load_raw(wt, a, slice(0, N), "wt_raw") for a in range(2)]
+        load_page(5)
         load_page(6)
         load_page(7)
-        wb_raw = ring.tile([P, 2, N], I32, name="wb_raw", tag="bf", bufs=3, align_bytes=64)
+        wb_raw = ring.tile([P, 2, N], I32, name="wb_raw", tag="raw", bufs=3, align_bytes=64)
         nc.sync.dma_start(out=wb_raw[:], in_=wb_words.rearrange("a p n t -> p a (n t)").bitcast(I32))
-        load_scales(nc.sync, wb_plane_raw, wb_scales)
+        load_scales(nc.gpsimd, wb_plane_raw, wb_scales)
         put_h1(0)
         put_h1(1)
-        quantise_wi(raws[0], 0, 1)
-        quantise_wi(raws[1], 1, 1)
-        put_h1(2)
-        put_h1(3)
+        quantise_wi(raws[0], 0, 1, 0)
+        quantise_wi(raws[1], 1, 1, 0)
         for k in range(5, 8):
             put_h2(k)
+        put_h1(2)
+        put_h1(3)
         product_a(1)
         for k in range(4, 8):
             put_h1(k)
@@ -323,8 +327,8 @@ def tile_list_blade_edge_register_kernel(
             if k % 2 == 1:
                 make_z_rows(k - 1, 0, PJ)
                 make_z_rows(k, 0, PJ)
-        quantise_z(0, 0, PJ // 2)
-        quantise_z(0, PJ // 2, PJ)
+        quantise_z(0, z_rows[0][:, :, 0:PASS], 0)
+        quantise_z(0, z_rows[0][:, :, PASS:PJ], PASS)
 
         y_all = keep.tile([P, PACK, PJ], F32, name="y_all", tag="at0")
         y_plane = keep.tile([P, PJ], U8, name="y_plane", align_bytes=64)
@@ -367,36 +371,52 @@ def tile_list_blade_edge_register_kernel(
             nc.sync.dma_start(out=y_words[:, j0 : j0 + CH], in_=y_codes[:].bitcast(I32))
 
         x_all = a_t[1][:].rearrange("p t h b m -> p t (h b m)")
-        z_rows[1] = keep.tile([P, PACK, PJ], BF16, name="z_rows1", tag="tab_w1", align_bytes=64)
+        late = keep.tile([P, 2, PACK, CH], F32, name="late", tag="tab_w1", align_bytes=64)
 
         s_early = keep.tile([P, 2, PACK, CH], F32, name="s_early", tag="tab_w0", align_bytes=64)
-        s_late = ring.tile([P, 2, PACK, CH], F32, name="s_late", tag="raw")
+        s_late = ring.tile([P, 2, PACK, CH], F32, name="s_late", tag="raw", bufs=3, align_bytes=64)
 
         def chunk_tiles(n):
-            x0 = CH * (n % 2)
-            return x_all[:, :, x0 : x0 + CH], (s_early if n < 2 else s_late)[:, n % 2, :, :]
+            x = late[:, 0, :, :] if n == 3 else x_all[:, :, CH * (n % 2) : CH * (n % 2 + 1)]
+            return x, (s_early if n < 2 else s_late)[:, n % 2, :, :]
+
+        def chunk_rows(n):
+            if n == 0:
+                return late[:, 0, :, :].bitcast(BF16)[:, :, 0:CH]
+            if n == 1:
+                return late[:, 1, :, :].bitcast(BF16)[:, :, 0:CH]
+            return x_all[:, :, n * CH : (n + 1) * CH].bitcast(BF16)[:, :, 0:CH]
 
         def fetch_chunk(n):
-            x, s = chunk_tiles(n)
+            x = chunk_tiles(n)[0]
             for t in range(PACK):
                 nc.vector.tensor_copy(x[:, t, :], pages[4 + t][:].indirect(l5[:, n * CH // 16 : (n + 1) * CH // 16]))
+
+        def sine_chunk(n):
+            x, s = chunk_tiles(n)
             nc.scalar.activation(s, x, ACT.Sin, bias=zero[:])
 
-        fetch_chunk(0)
-        fetch_chunk(1)
-        chunks = list(range(0, PJ, CH))
-        for n, j0 in enumerate(chunks):
-            jc = slice(j0, j0 + CH)
+        def make_z_chunk(n):
             x, s = chunk_tiles(n)
             nc.vector.tensor_tensor(s, x, s, ALU.add)
             for t in range(PACK):
-                nc.scalar.activation(z_rows[1][:, t, jc], s[:, t, :], ACT.Copy, scale=gain_t[:, 1, t : t + 1])
-            if n + 2 < len(chunks):
-                fetch_chunk(n + 2)
-            quantise_z(1, j0, j0 + CH)
-            if n >= 1:
-                second_stage(chunks[n - 1])
-        second_stage(chunks[-1])
+                nc.scalar.activation(chunk_rows(n)[:, t, :], s[:, t, :], ACT.Copy, scale=gain_t[:, 1, t : t + 1])
+            quantise_z(1, chunk_rows(n), n * CH)
+
+        for n in range(2):
+            fetch_chunk(n)
+            sine_chunk(n)
+        for n in range(2):
+            make_z_chunk(n)
+            fetch_chunk(n + 2)
+        second_stage(0)
+        sine_chunk(2)
+        make_z_chunk(2)
+        sine_chunk(3)
+        second_stage(CH)
+        make_z_chunk(3)
+        second_stage(2 * CH)
+        second_stage(3 * CH)
         for q in range(4):
             nc.sync.dma_start(
                 out=out_2[0, 4 * q : 4 * q + 4, :].bitcast(I32), in_=y_plane[32 * q : 32 * q + 4, :].bitcast(I32)

@@ -22,6 +22,7 @@ PACK = 4
 PASS = P * PACK
 CH = 256
 ON_PE = 4
+T0 = ON_PE - 4
 
 
 def tile_list_blade_edge_register_kernel(
@@ -88,10 +89,25 @@ def tile_list_blade_edge_register_kernel(
             nc.sync.dma_start(out=setpoints[k][:], in_=dealt_rows(sp, k // 4, k % 4))
 
         def load_wg(wg, name):
-            tile = keep.tile([P, PACK, S], F32, name=name)
+            rows = keep.tile([P, S], F32, name=name + "_rows", tag="wg_rows")
+            nc.sync.dma_start(out=rows[:], in_=wg)
+            return rows
+
+        def turn_wg(rows):
+            bank = psum.tile([P, 4, P], F32, name="wg_bank", tag="sp", bufs=2)
+            for jb in range(4):
+                nc.tensor.transpose(bank[:, jb, :], rows[:, P * jb : P * (jb + 1)], ident[:])
+            turned = keep.tile([P, PACK, 4, 4, 32], F32, name="wg_turned", tag="at1")
+            dealt = bank[:].rearrange("j b (m t) -> j t b m", t=PACK)
             for q in range(4):
-                nc.sync.dma_start(out=tile[32 * q : 32 * q + 32, :, :], in_=wg.rearrange("(p t) j -> p t j", t=PACK))
-            return tile
+                nc.scalar.copy(turned[:, :, :, q, :], dealt)
+            return turned
+
+        def deal_wg(turned, tile, t):
+            back = psum.tile([P, S], F32, name="wg_back", tag="h")
+            for jb in range(4):
+                nc.tensor.transpose(back[:, P * jb : P * (jb + 1)], turned[:, t, jb, :, :].rearrange("j q m -> j (q m)"), ident[:])
+            nc.scalar.copy(tile[:, t, :], back[:])
 
         def load_raw(w, a, cols, name):
             raw = ring.tile([P, PACK, PASS], F32, name=name, tag="raw", bufs=3, align_bytes=64)
@@ -110,6 +126,7 @@ def tile_list_blade_edge_register_kernel(
 
         l2 = load_list(offs2, "l2")
         l4 = load_list(offs4, "l4")
+        wg2_rows = load_wg(wg2, "wg2_t")
         load_scales(nc.sync, tab2_plane, tab2_scales)
         tab2_w = load_words(tab2_words, 0, "tab2_w", "tab2_w")
         wf_w = {}
@@ -123,8 +140,10 @@ def tile_list_blade_edge_register_kernel(
         make_identity(nc, ident[:])
         load_scales(nc.sync, wf_plane, wf_scales)
         load_sp(0)
-        wg2_t = load_wg(wg2, "wg2_t")
         load_page(0)
+        wg2_turned = turn_wg(wg2_rows)
+        wg2_t = keep.tile([P, PACK, S], F32, name="wg2_t")
+        deal_wg(wg2_turned, wg2_t, 0)
 
         v2 = gather(tab2_w, l2, U32, "v2")
         v2_plane = gather(tab2_plane, l2, U8, "v2_plane")
@@ -206,7 +225,6 @@ def tile_list_blade_edge_register_kernel(
             nc.scalar.copy(h1, bank[:])
             nc.vector.tensor_tensor(pages[k][:].indirect(l3[:]), h1, wg1_t[:, t, :], ALU.mult)
 
-        z_rows = {}
         x_t = {}
         s_t = {}
 
@@ -221,12 +239,6 @@ def tile_list_blade_edge_register_kernel(
 
         def make_z_rows(k, j0, j1):
             a, t = divmod(k, 4)
-            if a not in z_rows:
-                z_rows[a] = keep.tile([P, PACK, PJ], BF16, name="z_rows%d" % a, tag="tab_w%d" % a, align_bytes=64)
-            if k >= ON_PE:
-                nc.vector.tensor_tensor(s_t[k][:, j0:j1], x_t[k][:, j0:j1], s_t[k][:, j0:j1], ALU.add)
-                nc.scalar.activation(z_rows[a][:, t, j0:j1], s_t[k][:, j0:j1], ACT.Copy, scale=gain_t[:, a, t : t + 1])
-                return
             for h0 in range(j0, j1, PASS):
                 sum_bank = psum.tile([P, PASS], F32, name="sum_bank", tag="sp", bufs=2)
                 for jb in range(4):
@@ -237,7 +249,13 @@ def tile_list_blade_edge_register_kernel(
                 for jb in range(4):
                     jc = slice(h0 + P * jb, h0 + P * (jb + 1))
                     nc.tensor.transpose(back_bank[:, P * jb : P * (jb + 1)], x_t[k][:, jc], ident[:])
-                nc.scalar.activation(z_rows[a][:, t, h0 : h0 + PASS], back_bank[:], ACT.Copy, scale=gain_t[:, a, t : t + 1])
+                if a == 0:
+                    rows = z_rows0[:, t, h0 : h0 + PASS].rearrange("p (n c) -> p n c", n=2)
+                elif h0 == 0:
+                    rows = late[:, :, t, :].bitcast(BF16)[:, :, 0:CH]
+                else:
+                    rows = x_t[k][:, PASS:PJ].rearrange("p (n c) -> p n c", n=2).bitcast(BF16)[:, :, 0:CH]
+                nc.scalar.activation(rows, back_bank[:].rearrange("p (n c) -> p n c", n=2), ACT.Copy, scale=gain_t[:, a, t : t + 1])
 
         z_q = {}
 
@@ -254,28 +272,37 @@ def tile_list_blade_edge_register_kernel(
 
         product_f(0)
         put_h2(0)
+        deal_wg(wg2_turned, wg2_t, 1)
 
         load_sp(1)
         load_page(1)
+        wg1_rows = load_wg(wg1, "wg1_t")
         l1 = load_list(offs, "l1")
         load_scales(nc.gpsimd, tab_plane, tab_scales)
-        tab_w = [load_words(tab_words, c, "tab_w%d" % c, "tab_w%d" % c) for c in range(2)]
+        tab_w = [load_words(tab_words, 0, "tab_w0", "tab_w0")]
+        load_sp(2)
+        load_wf(1)
+        tab_w.append(load_words(tab_words, 1, "tab_w1", "tab_w1"))
+        load_sp(3)
+        raws = [load_raw(wi, 0, slice(0, PASS), "wi_raw")]
+        load_sp(4)
+        raws.append(load_raw(wi, 1, slice(0, PASS), "wi_raw"))
+        load_page(2)
+        load_page(3)
+        l3 = load_list(offs3, "l3")
+        load_page(4)
         put_h2(1)
         v_plane = gather(tab_plane, l1, U8, "v_plane")
         v = [gather(tab_w[c], l1, U32, "v%d" % c) for c in range(2)]
-        load_sp(2)
-        load_wf(1)
-        raws = [load_raw(wi, c, slice(0, PASS), "wi_raw") for c in range(2)]
-        load_sp(3)
-        load_page(2)
-        load_sp(4)
-        load_page(3)
-        l3 = load_list(offs3, "l3")
-        wg1_t = load_wg(wg1, "wg1_t")
-        load_page(4)
+        deal_wg(wg2_turned, wg2_t, 2)
+        deal_wg(wg2_turned, wg2_t, 3)
+        wg1_turned = turn_wg(wg1_rows)
+        wg1_t = keep.tile([P, PACK, S], F32, name="wg1_t")
+        for t in range(PACK):
+            deal_wg(wg1_turned, wg1_t, t)
         put_h2(2)
-        quantise_wi(raws[0], 0, 0, PASS)
-        quantise_wi(raws[1], 1, 0, PASS // 2)
+        quantise_wi(raws[0], 0, 0, 512)
+        quantise_wi(raws[1], 1, 0, 512)
         put_h2(3)
         product_f(1)
         put_h2(4)
@@ -283,16 +310,16 @@ def tile_list_blade_edge_register_kernel(
         l5 = load_list(offs5, "l5")
         gain_t = keep.tile([P, 2, PACK], F32, name="gain_t")
         nc.sync.dma_start(out=gain_t[:], in_=gain.rearrange("(a p t) -> p a t", a=2, t=PACK))
+
         raws = [load_raw(wi, c, slice(PASS, 2 * PASS), "wi_raw") for c in range(2)]
         for k in range(5, 8):
             load_sp(k)
         wt_raws = [load_raw(wt, a, slice(0, N), "wt_raw") for a in range(2)]
-        load_page(5)
-        load_page(6)
-        load_page(7)
+        for k in range(5, 8):
+            load_page(k)
         wb_raw = ring.tile([P, 2, N], I32, name="wb_raw", tag="raw", bufs=3, align_bytes=64)
         nc.sync.dma_start(out=wb_raw[:], in_=wb_words.rearrange("a p n t -> p a (n t)").bitcast(I32))
-        load_scales(nc.gpsimd, wb_plane_raw, wb_scales)
+        load_scales(nc.sync, wb_plane_raw, wb_scales)
         put_h1(0)
         put_h1(1)
         quantise_wi(raws[0], 0, 1, 0)
@@ -304,6 +331,8 @@ def tile_list_blade_edge_register_kernel(
         product_a(1)
         for k in range(4, 8):
             put_h1(k)
+        z_rows0 = keep.tile([P, PACK, PJ], BF16, name="z_rows0", tag="tab_w0", align_bytes=64)
+        late = keep.tile([P, 2, PACK, CH], F32, name="late", tag="tab_w1", align_bytes=64)
         wt_q = []
         for a in range(2):
             grouped = bf_tile(N * PACK, "wt_bf")
@@ -327,8 +356,8 @@ def tile_list_blade_edge_register_kernel(
             if k % 2 == 1:
                 make_z_rows(k - 1, 0, PJ)
                 make_z_rows(k, 0, PJ)
-        quantise_z(0, z_rows[0][:, :, 0:PASS], 0)
-        quantise_z(0, z_rows[0][:, :, PASS:PJ], PASS)
+        quantise_z(0, z_rows0[:, :, 0:PASS], 0)
+        quantise_z(0, z_rows0[:, :, PASS:PJ], PASS)
 
         y_all = keep.tile([P, PACK, PJ], F32, name="y_all", tag="at0")
         y_plane = keep.tile([P, PJ], U8, name="y_plane", align_bytes=64)
@@ -371,14 +400,13 @@ def tile_list_blade_edge_register_kernel(
             nc.sync.dma_start(out=y_words[:, j0 : j0 + CH], in_=y_codes[:].bitcast(I32))
 
         x_all = a_t[1][:].rearrange("p t h b m -> p t (h b m)")
-        late = keep.tile([P, 2, PACK, CH], F32, name="late", tag="tab_w1", align_bytes=64)
 
         s_early = keep.tile([P, 2, PACK, CH], F32, name="s_early", tag="tab_w0", align_bytes=64)
         s_late = ring.tile([P, 2, PACK, CH], F32, name="s_late", tag="raw", bufs=3, align_bytes=64)
 
         def chunk_tiles(n):
             x = late[:, 0, :, :] if n == 3 else x_all[:, :, CH * (n % 2) : CH * (n % 2 + 1)]
-            return x, (s_early if n < 2 else s_late)[:, n % 2, :, :]
+            return x[:, T0:, :], (s_early if n < 2 else s_late)[:, n % 2, T0:, :]
 
         def chunk_rows(n):
             if n == 0:
@@ -389,8 +417,8 @@ def tile_list_blade_edge_register_kernel(
 
         def fetch_chunk(n):
             x = chunk_tiles(n)[0]
-            for t in range(PACK):
-                nc.vector.tensor_copy(x[:, t, :], pages[4 + t][:].indirect(l5[:, n * CH // 16 : (n + 1) * CH // 16]))
+            for t in range(T0, PACK):
+                nc.vector.tensor_copy(x[:, t - T0, :], pages[4 + t][:].indirect(l5[:, n * CH // 16 : (n + 1) * CH // 16]))
 
         def sine_chunk(n):
             x, s = chunk_tiles(n)
@@ -399,8 +427,8 @@ def tile_list_blade_edge_register_kernel(
         def make_z_chunk(n):
             x, s = chunk_tiles(n)
             nc.vector.tensor_tensor(s, x, s, ALU.add)
-            for t in range(PACK):
-                nc.scalar.activation(chunk_rows(n)[:, t, :], s[:, t, :], ACT.Copy, scale=gain_t[:, 1, t : t + 1])
+            for t in range(T0, PACK):
+                nc.scalar.activation(chunk_rows(n)[:, t, :], s[:, t - T0, :], ACT.Copy, scale=gain_t[:, 1, t : t + 1])
             quantise_z(1, chunk_rows(n), n * CH)
 
         for n in range(2):

@@ -20,9 +20,15 @@ ALU = mybir.AluOpType
 P = 128
 PACK = 4
 PASS = P * PACK
-CH = 256
-ON_PE = 4
-T0 = ON_PE - 4
+QUADS = 4
+BLOCKS = PASS // P
+LINE = 4
+PER_COLUMN = 16
+CHUNK = 256
+RAW_BUFS = 3
+BF_BUFS = 3
+SMALL_BUFS = 8
+SIDE_BANKS = 2
 
 
 def tile_list_blade_edge_register_kernel(
@@ -36,83 +42,84 @@ def tile_list_blade_edge_register_kernel(
         ring = ctx.enter_context(tc.tile_pool(name="ring", bufs=2))
         psum = ctx.enter_context(tc.psum_pool(name="psum", bufs=3))
 
+        def block(jb):
+            return slice(P * jb, P * (jb + 1))
+
+        def side_bank(shape, name):
+            return psum.tile(shape, F32, name=name, tag="side", bufs=SIDE_BANKS)
+
+        def raw_tile(shape, dtype, name):
+            return ring.tile(shape, dtype, name=name, tag="raw", bufs=RAW_BUFS, align_bytes=64)
+
+        def small_tile(shape, dtype, name):
+            return ring.tile(shape, dtype, name=name, tag="small", bufs=SMALL_BUFS, align_bytes=64)
+
+        def bf_tile(width, name):
+            return ring.tile([P, width], BF16, name=name, tag="bf", bufs=BF_BUFS, align_bytes=64)
+
         def load_list(src, name):
             lst = keep.tile(list(src.shape), U16, name=name)
             nc.sync.dma_start(lst[:], src)
             return lst
 
-        def scale_plane(width, name):
+        def zeroed_plane(width, name):
             plane = keep.tile([P, width], U8, name=name, align_bytes=64)
             nc.vector.memset(plane[:].bitcast(I32), 0)
             return plane
 
-        def load_scales(queue, plane, scales):
+        def load_scales(plane, scales):
             passes = scales.shape[0]
-            for q in range(4):
-                queue.dma_start(
+            for q in range(QUADS):
+                nc.sync.dma_start(
                     out=plane[32 * q : 32 * q + 4 * passes, :].bitcast(I32),
                     in_=scales[:, 4 * q : 4 * q + 4, :].bitcast(I32),
                 )
 
-        def load_words(words, a, name, tag):
-            width = words.shape[2]
-            tile = keep.tile([P, width], U32, name=name, tag=tag, align_bytes=64)
-            nc.sync.dma_start(out=tile[:].bitcast(I32), in_=words[a].rearrange("p n t -> p (n t)").bitcast(I32))
+        def load_words(words, g, name):
+            tile = keep.tile([P, words.shape[2]], U32, name=name, tag=name, align_bytes=64)
+            nc.sync.dma_start(out=tile[:].bitcast(I32), in_=words[g].rearrange("p n t -> p (n t)").bitcast(I32))
             return tile
+
+        def dealt_rows(mat, k):
+            g, t = divmod(k, PACK)
+            return mat[PASS * g : PASS * (g + 1), :].rearrange("(p t) c -> p t c", t=PACK)[:, t, :]
+
+        pages = {}
+        setpoints = {}
+        wf_w = {}
+
+        def load_page(k):
+            pages[k] = keep.tile([P, T2], F32, name="page%d" % k)
+            nc.sync.dma_start(out=pages[k][:], in_=dealt_rows(page0, k))
+
+        def load_sp(k):
+            setpoints[k] = small_tile([P, S], F32, "sp%d" % k)
+            nc.sync.dma_start(out=setpoints[k][:], in_=dealt_rows(sp, k))
+
+        def load_wf(g):
+            wf_w[g] = keep.tile([P, 2 * PASS], U8, name="wf_w%d" % g, align_bytes=64)
+            nc.sync.dma_start(out=wf_w[g][:].bitcast(I32), in_=wf_words[0, :, 2 * PASS * g : 2 * PASS * (g + 1)].bitcast(I32))
+
+        def load_wg(wg, name):
+            rows = keep.tile([P, S], F32, name=name, tag="wg_rows")
+            nc.sync.dma_start(out=rows[:], in_=wg)
+            return rows
+
+        def load_weight(w, g, cols, name):
+            raw = raw_tile([P, PACK, PASS], F32, name)
+            nc.sync.dma_start(out=raw[:], in_=w[PASS * g : PASS * (g + 1), cols].rearrange("(p i) c -> p i c", i=PACK))
+            return raw
 
         def gather(src, lst, dtype, name):
             got = keep.tile([P, S], dtype, name=name, align_bytes=64)
             nc.vector.tensor_copy(got[:], src[:].indirect(lst[:]))
             return got
 
-        def dealt_rows(mat, a, t):
-            return mat[PASS * a : PASS * (a + 1), :].rearrange("(p t) c -> p t c", t=PACK)[:, t, :]
-
-        tab2_plane = scale_plane(TF, "tab2_plane")
-        wf_plane = scale_plane(H, "wf_plane")
-        zero_in = keep.tile([P, 1], F32, name="zero_in")
-        nc.vector.memset(zero_in[:], 0.0)
-        zero = keep.tile([P, 1], F32, name="zero")
-        nc.scalar.activation(zero[:], zero_in[:], ACT.Silu)
-        tab_plane = scale_plane(T, "tab_plane")
-        wb_plane_raw = scale_plane(N, "wb_plane_raw")
-
-        pages = {}
-        setpoints = {}
-
-        def load_page(k):
-            pages[k] = keep.tile([P, T2], F32, name="page%d" % k)
-            nc.sync.dma_start(out=pages[k][:], in_=dealt_rows(page0, k // 4, k % 4))
-
-        def load_sp(k):
-            setpoints[k] = ring.tile([P, S], F32, name="sp%d" % k, tag="sp", bufs=8, align_bytes=64)
-            nc.sync.dma_start(out=setpoints[k][:], in_=dealt_rows(sp, k // 4, k % 4))
-
-        def load_wg(wg, name):
-            rows = keep.tile([P, S], F32, name=name + "_rows", tag="wg_rows")
-            nc.sync.dma_start(out=rows[:], in_=wg)
-            return rows
-
-        def turn_wg(rows):
-            bank = psum.tile([P, 4, P], F32, name="wg_bank", tag="sp", bufs=2)
-            for jb in range(4):
-                nc.tensor.transpose(bank[:, jb, :], rows[:, P * jb : P * (jb + 1)], ident[:])
-            turned = keep.tile([P, PACK, 4, 4, 32], F32, name="wg_turned", tag="at1")
-            dealt = bank[:].rearrange("j b (m t) -> j t b m", t=PACK)
-            for q in range(4):
-                nc.scalar.copy(turned[:, :, :, q, :], dealt)
-            return turned
-
-        def deal_wg(turned, tile, t):
-            back = psum.tile([P, S], F32, name="wg_back", tag="h")
-            for jb in range(4):
-                nc.tensor.transpose(back[:, P * jb : P * (jb + 1)], turned[:, t, jb, :, :].rearrange("j q m -> j (q m)"), ident[:])
-            nc.scalar.copy(tile[:, t, :], back[:])
-
-        def load_raw(w, a, cols, name):
-            raw = ring.tile([P, PACK, PASS], F32, name=name, tag="raw", bufs=3, align_bytes=64)
-            nc.sync.dma_start(out=raw[:], in_=w[PASS * a : PASS * (a + 1), cols].rearrange("(p i) c -> p i c", i=PACK))
-            return raw
+        def interleave(copy, grouped, rows):
+            copy(
+                grouped.rearrange("p (c e t) -> p c t e", e=LINE, t=PACK),
+                rows.rearrange("p t (c e) -> p c t e", e=LINE),
+            )
 
         def quantise(grouped, name):
             width = grouped.shape[1] // PACK
@@ -121,315 +128,294 @@ def tile_list_blade_edge_register_kernel(
             nc.vector.quantize_mx(out=codes[:].bitcast(FP8X4), scales=plane[:], in_=grouped)
             return codes, plane
 
-        def bf_tile(width, name):
-            return ring.tile([P, width], BF16, name=name, tag="bf", bufs=3, align_bytes=64)
+        def add_transposed(out, first, second):
+            nc.tensor.matmul(out, first, ident[:], start=True, stop=False, is_transpose=True)
+            nc.tensor.matmul(out, second, ident[:], start=False, stop=True, is_transpose=True)
 
-        l2 = load_list(offs2, "l2")
-        l4 = load_list(offs4, "l4")
-        wg2_rows = load_wg(wg2, "wg2_t")
-        load_scales(nc.sync, tab2_plane, tab2_scales)
-        tab2_w = load_words(tab2_words, 0, "tab2_w", "tab2_w")
-        wf_w = {}
+        def turn_wg(rows):
+            bank = side_bank([P, BLOCKS, P], "wg_bank")
+            for jb in range(BLOCKS):
+                nc.tensor.transpose(bank[:, jb, :], rows[:, block(jb)], ident[:])
+            turned = keep.tile([P, PACK, BLOCKS, QUADS, 32], F32, name="wg_turned", tag="half1")
+            for q in range(QUADS):
+                nc.scalar.copy(turned[:, :, :, q, :], bank[:].rearrange("j b (m t) -> j t b m", t=PACK))
+            return turned
 
-        def load_wf(a):
-            wf_w[a] = keep.tile([P, 2 * PASS], U8, name="wf_w%d" % a, align_bytes=64)
-            nc.sync.dma_start(out=wf_w[a][:].bitcast(I32), in_=wf_words[0, :, 2 * PASS * a : 2 * PASS * (a + 1)].bitcast(I32))
-
-        load_wf(0)
-        ident = keep.tile([P, P], F32, name="ident")
-        make_identity(nc, ident[:])
-        load_scales(nc.sync, wf_plane, wf_scales)
-        load_sp(0)
-        load_page(0)
-        wg2_turned = turn_wg(wg2_rows)
-        wg2_t = keep.tile([P, PACK, S], F32, name="wg2_t")
-        deal_wg(wg2_turned, wg2_t, 0)
-
-        v2 = gather(tab2_w, l2, U32, "v2")
-        v2_plane = gather(tab2_plane, l2, U8, "v2_plane")
-
-        def add_transposed(bank, cols, first, second):
-            nc.tensor.matmul(bank[:, cols], first, ident[:], start=True, stop=False, is_transpose=True)
-            nc.tensor.matmul(bank[:, cols], second, ident[:], start=False, stop=True, is_transpose=True)
+        def deal_wg(turned, dealt, t):
+            bank = psum.tile([P, S], F32, name="wg_back", tag="turn")
+            for jb in range(BLOCKS):
+                nc.tensor.transpose(bank[:, block(jb)], turned[:, t, jb, :, :].rearrange("j q m -> j (q m)"), ident[:])
+            nc.scalar.copy(dealt[:, t, :], bank[:])
 
         f_t = {}
 
-        def product_f(a):
-            f_t[a] = keep.tile([P, PACK, 4, P], F32, name="f_t%d" % a, tag="at%d" % a)
-            for jb in range(4):
-                jc = slice(P * jb, P * (jb + 1))
+        def product_f(g, odd_copy):
+            f_t[g] = keep.tile([P, PACK, BLOCKS, P], F32, name="f_t%d" % g, tag="half%d" % g)
+            for jb in range(BLOCKS):
                 bank = psum.tile([P, PASS], F32, name="f_bank", tag="mx")
                 nc.tensor.matmul_mx(
-                    out=bank[:], lhsT=v2[:, jc].bitcast(FP8X4), lhsT_scale=v2_plane[:, jc],
-                    rhs=wf_w[a][:].bitcast(FP4X4),
-                    rhs_scale=wf_plane[:, PASS * a : PASS * (a + 1)], start=True, stop=True,
+                    out=bank[:], lhsT=v2[:, block(jb)].bitcast(FP8X4), lhsT_scale=v2_plane[:, block(jb)],
+                    rhs=wf_w[g][:].bitcast(FP4X4), rhs_scale=wf_plane[:, PASS * g : PASS * (g + 1)], start=True, stop=True,
                 )
-                dealt = bank[:].rearrange("j (m t) -> j t m", t=PACK)
-                if a == 0 and jb % 2 == 1:
-                    nc.vector.tensor_copy(f_t[a][:, :, jb, :], dealt)
-                else:
-                    nc.scalar.copy(f_t[a][:, :, jb, :], dealt)
+                copy = odd_copy if jb % 2 == 1 else nc.scalar.copy
+                copy(f_t[g][:, :, jb, :], bank[:].rearrange("j (m t) -> j t m", t=PACK))
 
         def put_h2(k):
-            a, t = divmod(k, 4)
-            sp_bank = psum.tile([P, S], F32, name="sp_bank", tag="sp", bufs=2)
-            for jb in range(4):
-                jc = slice(P * jb, P * (jb + 1))
-                nc.tensor.transpose(sp_bank[:, jc], setpoints[k][:, jc], ident[:])
-            neg_sp = setpoints[k]
-            nc.scalar.activation(neg_sp[:], sp_bank[:], ACT.Copy, scale=-1.0)
-            bank = psum.tile([P, S], F32, name="h2_bank", tag="h")
-            for jb in range(4):
-                jc = slice(P * jb, P * (jb + 1))
-                add_transposed(bank, jc, f_t[a][:, t, jb, :], neg_sp[:, jc])
-            h2 = setpoints[k]
-            nc.scalar.activation(h2[:], bank[:], ACT.Abs, bias=zero[:])
-            nc.vector.tensor_tensor(pages[k][:].indirect(l4[:]), h2[:], wg2_t[:, t, :], ALU.mult)
+            g, t = divmod(k, PACK)
+            held = setpoints[k]
+            sp_bank = side_bank([P, S], "sp_bank")
+            for jb in range(BLOCKS):
+                nc.tensor.transpose(sp_bank[:, block(jb)], held[:, block(jb)], ident[:])
+            nc.scalar.activation(held[:], sp_bank[:], ACT.Copy, scale=-1.0)
+            bank = psum.tile([P, S], F32, name="h2_bank", tag="turn")
+            for jb in range(BLOCKS):
+                add_transposed(bank[:, block(jb)], f_t[g][:, t, jb, :], held[:, block(jb)])
+            nc.scalar.activation(held[:], bank[:], ACT.Abs, bias=zero[:])
+            nc.vector.tensor_tensor(pages[k][:].indirect(list4[:]), held[:], wg2_dealt[:, t, :], ALU.mult)
 
         wi_q = {}
 
-        def quantise_wi(raw, c, a, on_vector):
+        def quantise_wi(raw, c, g, copy):
             grouped = bf_tile(PASS * PACK, "wi_bf")
-            dst = grouped[:].rearrange("p (c e i) -> p c i e", e=4, i=PACK)
-            src = raw[:].rearrange("p i (c e) -> p c i e", e=4)
-            split = on_vector // 4
-            if split > 0:
-                nc.vector.tensor_copy(dst[:, :split, :, :], src[:, :split, :, :])
-            if split < P:
-                nc.scalar.copy(dst[:, split:, :, :], src[:, split:, :, :])
-            wi_q[c, a] = quantise(grouped[:], "wi%d%d" % (c, a))
+            interleave(copy, grouped[:], raw[:])
+            wi_q[c, g] = quantise(grouped[:], "wi%d%d" % (c, g))
 
         a_t = {}
 
-        def product_a(a):
-            a_t[a] = keep.tile([P, PACK, 2, 4, P], F32, name="a_t%d" % a, tag="at%d" % a)
-            for jb in range(4):
-                jc = slice(P * jb, P * (jb + 1))
-                bank = psum.tile([P, PASS], F32, name="a_bank", tag=("mx", "h")[a])
+        def product_a(g, banks):
+            a_t[g] = keep.tile([P, PACK, 2, BLOCKS, P], F32, name="a_t%d" % g, tag="half%d" % g)
+            for jb in range(BLOCKS):
+                bank = psum.tile([P, PASS], F32, name="a_bank", tag=banks)
                 for c in range(2):
                     nc.tensor.matmul_mx(
-                        out=bank[:], lhsT=v[c][:, jc].bitcast(FP8X4), lhsT_scale=v_plane[4 * c : P, jc],
-                        rhs=wi_q[c, a][0][:].bitcast(FP8X4), rhs_scale=wi_q[c, a][1][:],
-                        start=(c == 0), stop=(c == 1),
+                        out=bank[:], lhsT=v[c][:, block(jb)].bitcast(FP8X4), lhsT_scale=v_plane[4 * c : P, block(jb)],
+                        rhs=wi_q[c, g][0][:].bitcast(FP8X4), rhs_scale=wi_q[c, g][1][:], start=(c == 0), stop=(c == 1),
                     )
-                dealt = bank[:].rearrange("j (m t) -> j t m", t=PACK)
-                nc.scalar.activation(a_t[a][:, :, 0, jb, :], dealt, ACT.Tanh, bias=zero[:])
-                nc.scalar.copy(a_t[a][:, :, 1, jb, :], dealt)
+                by_t = bank[:].rearrange("j (m t) -> j t m", t=PACK)
+                nc.scalar.activation(a_t[g][:, :, 0, jb, :], by_t, ACT.Tanh, bias=zero[:])
+                nc.scalar.copy(a_t[g][:, :, 1, jb, :], by_t)
 
         def put_h1(k):
-            a, t = divmod(k, 4)
-            bank = psum.tile([P, S], F32, name="h1_bank", tag="h")
-            for jb in range(4):
-                add_transposed(bank, slice(P * jb, P * (jb + 1)), a_t[a][:, t, 0, jb, :], a_t[a][:, t, 1, jb, :])
-            h1 = a_t[a][:, t, 0, :, :].rearrange("p b m -> p (b m)")
+            g, t = divmod(k, PACK)
+            bank = psum.tile([P, S], F32, name="h1_bank", tag="turn")
+            for jb in range(BLOCKS):
+                add_transposed(bank[:, block(jb)], a_t[g][:, t, 0, jb, :], a_t[g][:, t, 1, jb, :])
+            h1 = a_t[g][:, t, 0, :, :].rearrange("p b m -> p (b m)")
             nc.scalar.copy(h1, bank[:])
-            nc.vector.tensor_tensor(pages[k][:].indirect(l3[:]), h1, wg1_t[:, t, :], ALU.mult)
-
-        x_t = {}
-        s_t = {}
-
-        def fetch(k, j0, j1):
-            if j0 == 0:
-                x_t[k] = a_t[k // 4][:, k % 4, :, :, :].rearrange("p h b m -> p (h b m)")
-                if k % 2 == 0:
-                    s_t[k, 2] = ring.tile([P, 2, PJ], F32, name="s_pair", tag="raw", bufs=3, align_bytes=64)
-                s_t[k] = s_t[k - k % 2, 2][:, k % 2, :]
-            nc.vector.tensor_copy(x_t[k][:, j0:j1], pages[k][:].indirect(l5[:, j0 // 16 : j1 // 16]))
-            nc.scalar.activation(s_t[k][:, j0:j1], x_t[k][:, j0:j1], ACT.Sin, bias=zero[:])
-
-        def make_z_rows(k, j0, j1):
-            a, t = divmod(k, 4)
-            for h0 in range(j0, j1, PASS):
-                sum_bank = psum.tile([P, PASS], F32, name="sum_bank", tag="sp", bufs=2)
-                for jb in range(4):
-                    jc = slice(h0 + P * jb, h0 + P * (jb + 1))
-                    add_transposed(sum_bank, slice(P * jb, P * (jb + 1)), x_t[k][:, jc], s_t[k][:, jc])
-                nc.scalar.copy(x_t[k][:, h0 : h0 + PASS], sum_bank[:])
-                back_bank = psum.tile([P, PASS], F32, name="back_bank", tag="h")
-                for jb in range(4):
-                    jc = slice(h0 + P * jb, h0 + P * (jb + 1))
-                    nc.tensor.transpose(back_bank[:, P * jb : P * (jb + 1)], x_t[k][:, jc], ident[:])
-                if a == 0:
-                    rows = z_rows0[:, t, h0 : h0 + PASS].rearrange("p (n c) -> p n c", n=2)
-                elif h0 == 0:
-                    rows = late[:, :, t, :].bitcast(BF16)[:, :, 0:CH]
-                else:
-                    rows = x_t[k][:, PASS:PJ].rearrange("p (n c) -> p n c", n=2).bitcast(BF16)[:, :, 0:CH]
-                nc.scalar.activation(rows, back_bank[:].rearrange("p (n c) -> p n c", n=2), ACT.Copy, scale=gain_t[:, a, t : t + 1])
+            nc.vector.tensor_tensor(pages[k][:].indirect(list3[:]), h1, wg1_dealt[:, t, :], ALU.mult)
 
         z_q = {}
 
-        def quantise_z(a, rows, j0):
-            j1 = j0 + rows.shape[2]
-            grouped = bf_tile((j1 - j0) * PACK, "z_bf")
-            nc.scalar.copy(
-                grouped[:].rearrange("p (c e t) -> p c t e", e=4, t=PACK),
-                rows.rearrange("p t (c e) -> p c t e", e=4),
-            )
-            codes, plane = quantise(grouped[:], "z%d_%d" % (a, j0))
-            for j in range(j0, j1, CH):
-                z_q[a, j] = (codes[:, j - j0 : j - j0 + CH], plane[:, j - j0 : j - j0 + CH])
+        def quantise_z(g, rows, j0):
+            width = rows.shape[2]
+            grouped = bf_tile(width * PACK, "z_bf")
+            interleave(nc.scalar.copy, grouped[:], rows)
+            codes, plane = quantise(grouped[:], "z%d_%d" % (g, j0))
+            for j in range(0, width, P):
+                z_q[g, j0 + j] = (codes[:, j:], plane[:, j:])
 
-        product_f(0)
-        put_h2(0)
-        deal_wg(wg2_turned, wg2_t, 1)
+        tab2_plane = zeroed_plane(TF, "tab2_plane")
+        wf_plane = zeroed_plane(H, "wf_plane")
+        zero_in = keep.tile([P, 1], F32, name="zero_in")
+        nc.vector.memset(zero_in[:], 0.0)
+        zero = keep.tile([P, 1], F32, name="zero")
+        nc.scalar.activation(zero[:], zero_in[:], ACT.Silu)
+        tab_plane = zeroed_plane(T, "tab_plane")
+        wb_plane_raw = zeroed_plane(N, "wb_plane_raw")
 
+        list2 = load_list(offs2, "list2")
+        list4 = load_list(offs4, "list4")
+        wg2_rows = load_wg(wg2, "wg2_rows")
+        load_scales(tab2_plane, tab2_scales)
+        tab2_w = load_words(tab2_words, 0, "tab2_w")
+        load_wf(0)
+        ident = keep.tile([P, P], F32, name="ident")
+        make_identity(nc, ident[:])
+        load_scales(wf_plane, wf_scales)
+        load_sp(0)
+        list1 = load_list(offs, "list1")
+        tab_w = [load_words(tab_words, 0, "tab_w0")]
         load_sp(1)
-        load_page(1)
-        wg1_rows = load_wg(wg1, "wg1_t")
-        l1 = load_list(offs, "l1")
-        load_scales(nc.gpsimd, tab_plane, tab_scales)
-        tab_w = [load_words(tab_words, 0, "tab_w0", "tab_w0")]
-        load_sp(2)
-        load_wf(1)
-        tab_w.append(load_words(tab_words, 1, "tab_w1", "tab_w1"))
-        load_sp(3)
-        raws = [load_raw(wi, 0, slice(0, PASS), "wi_raw")]
-        load_sp(4)
-        raws.append(load_raw(wi, 1, slice(0, PASS), "wi_raw"))
-        load_page(2)
-        load_page(3)
-        l3 = load_list(offs3, "l3")
-        load_page(4)
-        put_h2(1)
-        v_plane = gather(tab_plane, l1, U8, "v_plane")
-        v = [gather(tab_w[c], l1, U32, "v%d" % c) for c in range(2)]
-        deal_wg(wg2_turned, wg2_t, 2)
-        deal_wg(wg2_turned, wg2_t, 3)
-        wg1_turned = turn_wg(wg1_rows)
-        wg1_t = keep.tile([P, PACK, S], F32, name="wg1_t")
-        for t in range(PACK):
-            deal_wg(wg1_turned, wg1_t, t)
-        put_h2(2)
-        quantise_wi(raws[0], 0, 0, 512)
-        quantise_wi(raws[1], 1, 0, 512)
-        put_h2(3)
-        product_f(1)
-        put_h2(4)
-        product_a(0)
-        l5 = load_list(offs5, "l5")
-        gain_t = keep.tile([P, 2, PACK], F32, name="gain_t")
-        nc.sync.dma_start(out=gain_t[:], in_=gain.rearrange("(a p t) -> p a t", a=2, t=PACK))
+        load_scales(tab_plane, tab_scales)
+        tab_w.append(load_words(tab_words, 1, "tab_w1"))
+        wg2_turned = turn_wg(wg2_rows)
+        wg1_rows = load_wg(wg1, "wg1_rows")
+        load_page(0)
+        wg2_dealt = keep.tile([P, PACK, S], F32, name="wg2_dealt")
+        deal_wg(wg2_turned, wg2_dealt, 0)
 
-        raws = [load_raw(wi, c, slice(PASS, 2 * PASS), "wi_raw") for c in range(2)]
-        for k in range(5, 8):
-            load_sp(k)
-        wt_raws = [load_raw(wt, a, slice(0, N), "wt_raw") for a in range(2)]
-        for k in range(5, 8):
-            load_page(k)
-        wb_raw = ring.tile([P, 2, N], I32, name="wb_raw", tag="raw", bufs=3, align_bytes=64)
-        nc.sync.dma_start(out=wb_raw[:], in_=wb_words.rearrange("a p n t -> p a (n t)").bitcast(I32))
-        load_scales(nc.sync, wb_plane_raw, wb_scales)
+        v2 = gather(tab2_w, list2, U32, "v2")
+        v2_plane = gather(tab2_plane, list2, U8, "v2_plane")
+        product_f(0, nc.vector.tensor_copy)
+        put_h2(0)
+        deal_wg(wg2_turned, wg2_dealt, 1)
+
+        load_sp(2)
+        wi_raw = [load_weight(wi, 0, slice(0, PASS), "wi_raw")]
+        load_sp(3)
+        wi_raw.append(load_weight(wi, 1, slice(0, PASS), "wi_raw"))
+        load_page(1)
+        load_page(2)
+        list3 = load_list(offs3, "list3")
+        load_page(3)
+        load_wf(1)
+        load_sp(4)
+        load_page(4)
+
+        put_h2(1)
+        v_plane = gather(tab_plane, list1, U8, "v_plane")
+        v = [gather(tab_w[c], list1, U32, "v%d" % c) for c in range(2)]
+        deal_wg(wg2_turned, wg2_dealt, 2)
+        deal_wg(wg2_turned, wg2_dealt, 3)
+        wg1_turned = turn_wg(wg1_rows)
+        wg1_dealt = keep.tile([P, PACK, S], F32, name="wg1_dealt")
+        for t in range(PACK):
+            deal_wg(wg1_turned, wg1_dealt, t)
+        put_h2(2)
+        for c in range(2):
+            quantise_wi(wi_raw[c], c, 0, nc.vector.tensor_copy)
+        put_h2(3)
+        product_a(0, "mx")
         put_h1(0)
         put_h1(1)
-        quantise_wi(raws[0], 0, 1, 0)
-        quantise_wi(raws[1], 1, 1, 0)
+        product_f(1, nc.scalar.copy)
+        put_h2(4)
+
+        list5 = load_list(offs5, "list5")
+        gain_dealt = keep.tile([P, 2, PACK], F32, name="gain_dealt")
+        nc.sync.dma_start(out=gain_dealt[:], in_=gain.rearrange("(g p t) -> p g t", g=2, t=PACK))
+        wi_raw = [load_weight(wi, c, slice(PASS, 2 * PASS), "wi_raw") for c in range(2)]
+        for k in range(5, 8):
+            load_sp(k)
+        wt_raw = [load_weight(wt, g, slice(0, N), "wt_raw") for g in range(2)]
+        for k in range(5, 8):
+            load_page(k)
+        wb_raw = raw_tile([P, 2, N], I32, "wb_raw")
+        nc.sync.dma_start(out=wb_raw[:], in_=wb_words.rearrange("g p n t -> p g (n t)").bitcast(I32))
+        load_scales(wb_plane_raw, wb_scales)
+
+        for c in range(2):
+            quantise_wi(wi_raw[c], c, 1, nc.scalar.copy)
         for k in range(5, 8):
             put_h2(k)
         put_h1(2)
         put_h1(3)
-        product_a(1)
+        product_a(1, "turn")
         for k in range(4, 8):
             put_h1(k)
+
         z_rows0 = keep.tile([P, PACK, PJ], BF16, name="z_rows0", tag="tab_w0", align_bytes=64)
-        late = keep.tile([P, 2, PACK, CH], F32, name="late", tag="tab_w1", align_bytes=64)
+        spare = keep.tile([P, 2, PACK, CHUNK], F32, name="spare", tag="tab_w1", align_bytes=64)
         wt_q = []
-        for a in range(2):
+        for g in range(2):
             grouped = bf_tile(N * PACK, "wt_bf")
             nc.scalar.copy(
                 grouped[:].rearrange("p (t m i) -> p m i t", t=PACK, i=PACK),
-                wt_raws[a][:].rearrange("p i (m t) -> p m i t", t=PACK),
+                wt_raw[g][:].rearrange("p i (m t) -> p m i t", t=PACK),
             )
-            wt_q.append(quantise(grouped[:], "wt%d" % a))
+            wt_q.append(quantise(grouped[:], "wt%d" % g))
         wb_w = keep.tile([P, 2, N], U32, name="wb_w", tag="tab2_w", align_bytes=64)
         wb_plane = keep.tile([P, N], U8, name="wb_plane", align_bytes=64)
         nc.vector.tensor_copy(
-            wb_w[:].bitcast(I32).rearrange("p a (t m) -> p a m t", t=PACK),
-            wb_raw[:].rearrange("p a (m t) -> p a m t", t=PACK),
+            wb_w[:].bitcast(I32).rearrange("p g (t m) -> p g m t", t=PACK),
+            wb_raw[:].rearrange("p g (m t) -> p g m t", t=PACK),
         )
         nc.vector.tensor_copy(
             wb_plane[:].rearrange("p (t m) -> p t m", t=PACK),
             wb_plane_raw[:].rearrange("p (m t) -> p t m", t=PACK),
         )
-        for k in range(4):
-            fetch(k, 0, PJ)
-            if k % 2 == 1:
-                make_z_rows(k - 1, 0, PJ)
-                make_z_rows(k, 0, PJ)
-        quantise_z(0, z_rows0[:, :, 0:PASS], 0)
-        quantise_z(0, z_rows0[:, :, PASS:PJ], PASS)
+        wb_q = [(wb_w[:, g, :], wb_plane[4 * g : P, :]) for g in range(2)]
 
-        y_all = keep.tile([P, PACK, PJ], F32, name="y_all", tag="at0")
+        x_of = [a_t[g][:].rearrange("p t h b m -> p t (h b m)") for g in range(2)]
+        for pair in range(2):
+            sines = raw_tile([P, 2, PJ], F32, "sines")
+            for e in range(2):
+                t = 2 * pair + e
+                nc.vector.tensor_copy(x_of[0][:, t, :], pages[t][:].indirect(list5[:]))
+                nc.scalar.activation(sines[:, e, :], x_of[0][:, t, :], ACT.Sin, bias=zero[:])
+            for e in range(2):
+                t = 2 * pair + e
+                for j0 in range(0, PJ, PASS):
+                    x = x_of[0][:, t, j0 : j0 + PASS]
+                    sum_bank = side_bank([P, PASS], "sum_bank")
+                    for jb in range(BLOCKS):
+                        add_transposed(sum_bank[:, block(jb)], x[:, block(jb)], sines[:, e, j0 : j0 + PASS][:, block(jb)])
+                    nc.scalar.copy(x, sum_bank[:])
+                    back_bank = psum.tile([P, PASS], F32, name="back_bank", tag="turn")
+                    for jb in range(BLOCKS):
+                        nc.tensor.transpose(back_bank[:, block(jb)], x[:, block(jb)], ident[:])
+                    nc.scalar.activation(
+                        z_rows0[:, t, j0 : j0 + PASS], back_bank[:], ACT.Copy, scale=gain_dealt[:, 0, t : t + 1]
+                    )
+        for j0 in range(0, PJ, PASS):
+            quantise_z(0, z_rows0[:, :, j0 : j0 + PASS], j0)
+
+        y_all = keep.tile([P, PACK, PJ], F32, name="y_all", tag="half0")
         y_plane = keep.tile([P, PJ], U8, name="y_plane", align_bytes=64)
         y_rows = out_0.rearrange("(p t) j -> p t j", t=PACK)
         y_words = out_1[0].rearrange("p m t -> p (m t)").bitcast(I32)
 
-        def second_stage(j0):
-            y = y_all[:, :, j0 : j0 + CH]
+        def product_z(bank, weight, u, j0, width):
+            for e in range(2):
+                for g in range(2):
+                    codes, plane = weight[g]
+                    nc.tensor.matmul_mx(
+                        out=bank[:, e, :], lhsT=codes[:, block(2 * u + e)].bitcast(FP8X4), lhsT_scale=plane[:, block(2 * u + e)],
+                        rhs=z_q[g, j0][0][:, :width].bitcast(FP8X4), rhs_scale=z_q[g, j0][1][:, :width],
+                        start=(g == 0), stop=(g == 1),
+                    )
+
+        def second_stage(j0, width):
+            y = y_all[:, :, j0 : j0 + width]
             for u in range(2):
                 if u == 0:
-                    e_bank = psum.tile([P, 2, CH], F32, name="e_bank", tag="mx")
+                    e_bank = psum.tile([P, 2, width], F32, name="e_bank", tag="mx")
                 else:
-                    e_bank = psum.tile([P, 2, CH], F32, name="e_bank", tag="sp", bufs=2)
-                b_bank = psum.tile([P, 2, CH], F32, name="b_bank", tag="h")
-                for e in range(2):
-                    nc_cols = slice(P * (2 * u + e), P * (2 * u + e + 1))
-                    for a in range(2):
-                        nc.tensor.matmul_mx(
-                            out=e_bank[:, e, :], lhsT=wt_q[a][0][:, nc_cols].bitcast(FP8X4), lhsT_scale=wt_q[a][1][:, nc_cols],
-                            rhs=z_q[a, j0][0].bitcast(FP8X4), rhs_scale=z_q[a, j0][1], start=(a == 0), stop=(a == 1),
-                        )
-                for e in range(2):
-                    nc_cols = slice(P * (2 * u + e), P * (2 * u + e + 1))
-                    for a in range(2):
-                        nc.tensor.matmul_mx(
-                            out=b_bank[:, e, :], lhsT=wb_w[:, a, nc_cols].bitcast(FP8X4), lhsT_scale=wb_plane[4 * a : P, nc_cols],
-                            rhs=z_q[a, j0][0].bitcast(FP8X4), rhs_scale=z_q[a, j0][1], start=(a == 0), stop=(a == 1),
-                        )
-                tanh_e = ring.tile([P, 2, CH], F32, name="tanh_e", tag="sp", bufs=8, align_bytes=64)
+                    e_bank = side_bank([P, 2, width], "e_bank")
+                b_bank = psum.tile([P, 2, width], F32, name="b_bank", tag="turn")
+                product_z(e_bank, wt_q, u, j0, width)
+                product_z(b_bank, wb_q, u, j0, width)
+                tanh_e = small_tile([P, 2, width], F32, "tanh_e")
                 nc.scalar.activation(tanh_e[:], e_bank[:], ACT.Tanh, bias=zero[:])
                 nc.vector.tensor_tensor(y[:, 2 * u : 2 * u + 2, :], b_bank[:], tanh_e[:], ALU.add)
-            nc.sync.dma_start(out=y_rows[:, :, j0 : j0 + CH], in_=y)
-            y_bf = ring.tile([P, CH * PACK], BF16, name="y_bf", tag="sp", bufs=8, align_bytes=64)
-            nc.vector.tensor_copy(
-                y_bf[:].rearrange("p (c e t) -> p c t e", e=4, t=PACK),
-                y.rearrange("p t (c e) -> p c t e", e=4),
-            )
-            y_codes = keep.tile([P, CH], U32, name="y_codes%d" % j0, align_bytes=64)
-            nc.vector.quantize_mx(out=y_codes[:].bitcast(FP8X4), scales=y_plane[:, j0 : j0 + CH], in_=y_bf[:])
-            nc.sync.dma_start(out=y_words[:, j0 : j0 + CH], in_=y_codes[:].bitcast(I32))
+            nc.sync.dma_start(out=y_rows[:, :, j0 : j0 + width], in_=y)
+            y_bf = small_tile([P, width * PACK], BF16, "y_bf")
+            interleave(nc.vector.tensor_copy, y_bf[:], y)
+            y_codes = keep.tile([P, width], U32, name="y_codes%d" % j0, align_bytes=64)
+            nc.vector.quantize_mx(out=y_codes[:].bitcast(FP8X4), scales=y_plane[:, j0 : j0 + width], in_=y_bf[:])
+            nc.sync.dma_start(out=y_words[:, j0 : j0 + width], in_=y_codes[:].bitcast(I32))
 
-        x_all = a_t[1][:].rearrange("p t h b m -> p t (h b m)")
+        sines_early = keep.tile([P, 2, PACK, CHUNK], F32, name="sines_early", tag="tab_w0", align_bytes=64)
+        sines_late = raw_tile([P, 2, PACK, CHUNK], F32, "sines_late")
+        x_cols = [x_of[1][:, :, n * CHUNK : (n + 1) * CHUNK] for n in range(PJ // CHUNK)]
+        chunk_x = [x_cols[0], x_cols[1], x_cols[0], spare[:, 0, :, :]]
+        chunk_sines = [sines_early[:, 0, :, :], sines_early[:, 1, :, :], sines_late[:, 0, :, :], sines_late[:, 1, :, :]]
+        chunk_rows = [place.bitcast(BF16)[:, :, 0:CHUNK] for place in (spare[:, 0, :, :], spare[:, 1, :, :], x_cols[2], x_cols[3])]
 
-        s_early = keep.tile([P, 2, PACK, CH], F32, name="s_early", tag="tab_w0", align_bytes=64)
-        s_late = ring.tile([P, 2, PACK, CH], F32, name="s_late", tag="raw", bufs=3, align_bytes=64)
-
-        def chunk_tiles(n):
-            x = late[:, 0, :, :] if n == 3 else x_all[:, :, CH * (n % 2) : CH * (n % 2 + 1)]
-            return x[:, T0:, :], (s_early if n < 2 else s_late)[:, n % 2, T0:, :]
-
-        def chunk_rows(n):
-            if n == 0:
-                return late[:, 0, :, :].bitcast(BF16)[:, :, 0:CH]
-            if n == 1:
-                return late[:, 1, :, :].bitcast(BF16)[:, :, 0:CH]
-            return x_all[:, :, n * CH : (n + 1) * CH].bitcast(BF16)[:, :, 0:CH]
+        def pieces(n):
+            width = P if n == PJ // CHUNK - 1 else CHUNK
+            return [(j0, width) for j0 in range(n * CHUNK, (n + 1) * CHUNK, width)]
 
         def fetch_chunk(n):
-            x = chunk_tiles(n)[0]
-            for t in range(T0, PACK):
-                nc.vector.tensor_copy(x[:, t - T0, :], pages[4 + t][:].indirect(l5[:, n * CH // 16 : (n + 1) * CH // 16]))
+            entries = list5[:, n * CHUNK // PER_COLUMN : (n + 1) * CHUNK // PER_COLUMN]
+            for t in range(PACK):
+                nc.vector.tensor_copy(chunk_x[n][:, t, :], pages[PACK + t][:].indirect(entries))
 
         def sine_chunk(n):
-            x, s = chunk_tiles(n)
-            nc.scalar.activation(s, x, ACT.Sin, bias=zero[:])
+            nc.scalar.activation(chunk_sines[n], chunk_x[n], ACT.Sin, bias=zero[:])
 
         def make_z_chunk(n):
-            x, s = chunk_tiles(n)
-            nc.vector.tensor_tensor(s, x, s, ALU.add)
-            for t in range(T0, PACK):
-                nc.scalar.activation(chunk_rows(n)[:, t, :], s[:, t - T0, :], ACT.Copy, scale=gain_t[:, 1, t : t + 1])
-            quantise_z(1, chunk_rows(n), n * CH)
+            nc.vector.tensor_tensor(chunk_sines[n], chunk_x[n], chunk_sines[n], ALU.add)
+            for t in range(PACK):
+                nc.scalar.activation(
+                    chunk_rows[n][:, t, :], chunk_sines[n][:, t, :], ACT.Copy, scale=gain_dealt[:, 1, t : t + 1]
+                )
+            for j0, width in pieces(n):
+                quantise_z(1, chunk_rows[n][:, :, j0 - n * CHUNK : j0 - n * CHUNK + width], j0)
+
+        def finish_chunk(n):
+            for j0, width in pieces(n):
+                second_stage(j0, width)
 
         for n in range(2):
             fetch_chunk(n)
@@ -437,15 +423,15 @@ def tile_list_blade_edge_register_kernel(
         for n in range(2):
             make_z_chunk(n)
             fetch_chunk(n + 2)
-        second_stage(0)
+        finish_chunk(0)
         sine_chunk(2)
         make_z_chunk(2)
         sine_chunk(3)
-        second_stage(CH)
+        finish_chunk(1)
         make_z_chunk(3)
-        second_stage(2 * CH)
-        second_stage(3 * CH)
-        for q in range(4):
+        finish_chunk(2)
+        finish_chunk(3)
+        for q in range(QUADS):
             nc.sync.dma_start(
                 out=out_2[0, 4 * q : 4 * q + 4, :].bitcast(I32), in_=y_plane[32 * q : 32 * q + 4, :].bitcast(I32)
             )

from contextlib import ExitStack

import concourse.mybir as mybir
from concourse.masks import make_identity

K, M, H, N, T, TF, S, T2, PJ = 1024, 512, 1024, 512, 2048, 1024, 512, 2048, 1024
FLOPS = 2 * (K * H * S + M * H * S + 2 * H * N * PJ)

F32 = mybir.dt.float32
BF16 = mybir.dt.bfloat16
I32 = mybir.dt.int32
U32 = mybir.dt.uint32
U16 = mybir.dt.uint16
U8 = mybir.dt.uint8
FP8X4 = mybir.dt.float8_e4m3fn_x4
FP4X4 = mybir.dt.float4_e2m1fn_x4
ACT = mybir.ActivationFunctionType
ALU = mybir.AluOpType

P = 128
PACK = 4
PASS = P * PACK
QUADS = 4
BLOCKS = PASS // P
LINE = 4
PER_COLUMN = 16
CHUNK = 256
RAW_BUFS = 3
BF_BUFS = 3
SMALL_BUFS = 8
SIDE_BANKS = 2


def tile_list_blade_edge_register_kernel(
    tc, tab_words, tab_scales, tab2_words, tab2_scales, offs, offs2, offs3, offs4, offs5,
    wi, wf_words, wf_scales, sp, wg1, wg2, page0, gain, wt, wb_words, wb_scales,
    out_0, out_1, out_2,
):
    nc = tc.nc
    with ExitStack() as ctx:
        keep = ctx.enter_context(tc.tile_pool(name="keep", bufs=1))
        ring = ctx.enter_context(tc.tile_pool(name="ring", bufs=2))
        psum = ctx.enter_context(tc.psum_pool(name="psum", bufs=3))

        def block(jb):
            return slice(P * jb, P * (jb + 1))

        def side_bank(shape, name):
            return psum.tile(shape, F32, name=name, tag="side", bufs=SIDE_BANKS)

        def raw_tile(shape, dtype, name):
            return ring.tile(shape, dtype, name=name, tag="raw", bufs=RAW_BUFS, align_bytes=64)

        def small_tile(shape, dtype, name):
            return ring.tile(shape, dtype, name=name, tag="small", bufs=SMALL_BUFS, align_bytes=64)

        def bf_tile(width, name):
            return ring.tile([P, width], BF16, name=name, tag="bf", bufs=BF_BUFS, align_bytes=64)

        def load_list(src, name):
            lst = keep.tile(list(src.shape), U16, name=name)
            nc.sync.dma_start(lst[:], src)
            return lst

        def zeroed_plane(width, name):
            plane = keep.tile([P, width], U8, name=name, align_bytes=64)
            nc.vector.memset(plane[:].bitcast(I32), 0)
            return plane

        def load_scales(plane, scales):
            passes = scales.shape[0]
            for q in range(QUADS):
                nc.sync.dma_start(
                    out=plane[32 * q : 32 * q + 4 * passes, :].bitcast(I32),
                    in_=scales[:, 4 * q : 4 * q + 4, :].bitcast(I32),
                )

        def load_words(words, g, name):
            tile = keep.tile([P, words.shape[2]], U32, name=name, tag=name, align_bytes=64)
            nc.sync.dma_start(out=tile[:].bitcast(I32), in_=words[g].rearrange("p n t -> p (n t)").bitcast(I32))
            return tile

        def dealt_rows(mat, k):
            g, t = divmod(k, PACK)
            return mat[PASS * g : PASS * (g + 1), :].rearrange("(p t) c -> p t c", t=PACK)[:, t, :]

        pages = {}
        setpoints = {}
        wf_w = {}

        def load_page(k):
            pages[k] = keep.tile([P, T2], F32, name="page%d" % k)
            nc.sync.dma_start(out=pages[k][:], in_=dealt_rows(page0, k))

        def load_sp(k):
            setpoints[k] = small_tile([P, S], F32, "sp%d" % k)
            nc.sync.dma_start(out=setpoints[k][:], in_=dealt_rows(sp, k))

        def load_wf(g):
            wf_w[g] = keep.tile([P, 2 * PASS], U8, name="wf_w%d" % g, align_bytes=64)
            nc.sync.dma_start(out=wf_w[g][:].bitcast(I32), in_=wf_words[0, :, 2 * PASS * g : 2 * PASS * (g + 1)].bitcast(I32))

        def load_wg(wg, name):
            rows = keep.tile([P, S], F32, name=name, tag="wg_rows")
            nc.sync.dma_start(out=rows[:], in_=wg)
            return rows

        def load_weight(w, g, cols, name):
            raw = raw_tile([P, PACK, PASS], F32, name)
            nc.sync.dma_start(out=raw[:], in_=w[PASS * g : PASS * (g + 1), cols].rearrange("(p i) c -> p i c", i=PACK))
            return raw

        def gather(src, lst, dtype, name):
            got = keep.tile([P, S], dtype, name=name, align_bytes=64)
            nc.vector.tensor_copy(got[:], src[:].indirect(lst[:]))
            return got

        def interleave(copy, grouped, rows):
            copy(
                grouped.rearrange("p (c e t) -> p c t e", e=LINE, t=PACK),
                rows.rearrange("p t (c e) -> p c t e", e=LINE),
            )

        def quantise(grouped, name):
            width = grouped.shape[1] // PACK
            codes = keep.tile([P, width], U32, name=name + "_codes", align_bytes=64)
            plane = keep.tile([P, width], U8, name=name + "_plane", align_bytes=64)
            nc.vector.quantize_mx(out=codes[:].bitcast(FP8X4), scales=plane[:], in_=grouped)
            return codes, plane

        def add_transposed(out, first, second):
            nc.tensor.matmul(out, first, ident[:], start=True, stop=False, is_transpose=True)
            nc.tensor.matmul(out, second, ident[:], start=False, stop=True, is_transpose=True)

        def turn_wg(rows):
            bank = side_bank([P, BLOCKS, P], "wg_bank")
            for jb in range(BLOCKS):
                nc.tensor.transpose(bank[:, jb, :], rows[:, block(jb)], ident[:])
            turned = keep.tile([P, PACK, BLOCKS, QUADS, 32], F32, name="wg_turned", tag="half1")
            for q in range(QUADS):
                nc.scalar.copy(turned[:, :, :, q, :], bank[:].rearrange("j b (m t) -> j t b m", t=PACK))
            return turned

        def deal_wg(turned, dealt, t):
            bank = psum.tile([P, S], F32, name="wg_back", tag="turn")
            for jb in range(BLOCKS):
                nc.tensor.transpose(bank[:, block(jb)], turned[:, t, jb, :, :].rearrange("j q m -> j (q m)"), ident[:])
            nc.scalar.copy(dealt[:, t, :], bank[:])

        f_t = {}

        def product_f(g, odd_copy):
            f_t[g] = keep.tile([P, PACK, BLOCKS, P], F32, name="f_t%d" % g, tag="half%d" % g)
            for jb in range(BLOCKS):
                bank = psum.tile([P, PASS], F32, name="f_bank", tag="mx")
                nc.tensor.matmul_mx(
                    out=bank[:], lhsT=v2[:, block(jb)].bitcast(FP8X4), lhsT_scale=v2_plane[:, block(jb)],
                    rhs=wf_w[g][:].bitcast(FP4X4), rhs_scale=wf_plane[:, PASS * g : PASS * (g + 1)], start=True, stop=True,
                )
                copy = odd_copy if jb % 2 == 1 else nc.scalar.copy
                copy(f_t[g][:, :, jb, :], bank[:].rearrange("j (m t) -> j t m", t=PACK))

        def put_h2(k):
            g, t = divmod(k, PACK)
            held = setpoints[k]
            sp_bank = side_bank([P, S], "sp_bank")
            for jb in range(BLOCKS):
                nc.tensor.transpose(sp_bank[:, block(jb)], held[:, block(jb)], ident[:])
            nc.scalar.activation(held[:], sp_bank[:], ACT.Copy, scale=-1.0)
            bank = psum.tile([P, S], F32, name="h2_bank", tag="turn")
            for jb in range(BLOCKS):
                add_transposed(bank[:, block(jb)], f_t[g][:, t, jb, :], held[:, block(jb)])
            nc.scalar.activation(held[:], bank[:], ACT.Abs, bias=zero[:])
            nc.vector.tensor_tensor(pages[k][:].indirect(list4[:]), held[:], wg2_dealt[:, t, :], ALU.mult)

        wi_q = {}

        def quantise_wi(raw, c, g, copy):
            grouped = bf_tile(PASS * PACK, "wi_bf")
            interleave(copy, grouped[:], raw[:])
            wi_q[c, g] = quantise(grouped[:], "wi%d%d" % (c, g))

        a_t = {}

        def product_a(g, banks):
            a_t[g] = keep.tile([P, PACK, 2, BLOCKS, P], F32, name="a_t%d" % g, tag="half%d" % g)
            for jb in range(BLOCKS):
                bank = psum.tile([P, PASS], F32, name="a_bank", tag=banks)
                for c in range(2):
                    nc.tensor.matmul_mx(
                        out=bank[:], lhsT=v[c][:, block(jb)].bitcast(FP8X4), lhsT_scale=v_plane[4 * c : P, block(jb)],
                        rhs=wi_q[c, g][0][:].bitcast(FP8X4), rhs_scale=wi_q[c, g][1][:], start=(c == 0), stop=(c == 1),
                    )
                by_t = bank[:].rearrange("j (m t) -> j t m", t=PACK)
                nc.scalar.activation(a_t[g][:, :, 0, jb, :], by_t, ACT.Tanh, bias=zero[:])
                nc.scalar.copy(a_t[g][:, :, 1, jb, :], by_t)

        def put_h1(k):
            g, t = divmod(k, PACK)
            bank = psum.tile([P, S], F32, name="h1_bank", tag="turn")
            for jb in range(BLOCKS):
                add_transposed(bank[:, block(jb)], a_t[g][:, t, 0, jb, :], a_t[g][:, t, 1, jb, :])
            h1 = a_t[g][:, t, 0, :, :].rearrange("p b m -> p (b m)")
            nc.scalar.copy(h1, bank[:])
            nc.vector.tensor_tensor(pages[k][:].indirect(list3[:]), h1, wg1_dealt[:, t, :], ALU.mult)

        z_q = {}

        def quantise_z(g, rows, j0):
            width = rows.shape[2]
            grouped = bf_tile(width * PACK, "z_bf")
            interleave(nc.scalar.copy, grouped[:], rows)
            codes, plane = quantise(grouped[:], "z%d_%d" % (g, j0))
            for j in range(0, width, P):
                z_q[g, j0 + j] = (codes[:, j:], plane[:, j:])

        tab2_plane = zeroed_plane(TF, "tab2_plane")
        wf_plane = zeroed_plane(H, "wf_plane")
        zero_in = keep.tile([P, 1], F32, name="zero_in")
        nc.vector.memset(zero_in[:], 0.0)
        zero = keep.tile([P, 1], F32, name="zero")
        nc.scalar.activation(zero[:], zero_in[:], ACT.Silu)
        tab_plane = zeroed_plane(T, "tab_plane")
        wb_plane_raw = zeroed_plane(N, "wb_plane_raw")

        list2 = load_list(offs2, "list2")
        list4 = load_list(offs4, "list4")
        wg2_rows = load_wg(wg2, "wg2_rows")
        load_scales(tab2_plane, tab2_scales)
        tab2_w = load_words(tab2_words, 0, "tab2_w")
        load_wf(0)
        ident = keep.tile([P, P], F32, name="ident")
        make_identity(nc, ident[:])
        load_scales(wf_plane, wf_scales)
        load_sp(0)
        list1 = load_list(offs, "list1")
        tab_w = [load_words(tab_words, 0, "tab_w0")]
        load_sp(1)
        load_scales(tab_plane, tab_scales)
        tab_w.append(load_words(tab_words, 1, "tab_w1"))
        wg2_turned = turn_wg(wg2_rows)
        wg1_rows = load_wg(wg1, "wg1_rows")
        load_page(0)
        wg2_dealt = keep.tile([P, PACK, S], F32, name="wg2_dealt")
        deal_wg(wg2_turned, wg2_dealt, 0)

        v2 = gather(tab2_w, list2, U32, "v2")
        v2_plane = gather(tab2_plane, list2, U8, "v2_plane")
        product_f(0, nc.vector.tensor_copy)
        put_h2(0)
        deal_wg(wg2_turned, wg2_dealt, 1)

        load_sp(2)
        wi_raw = [load_weight(wi, 0, slice(0, PASS), "wi_raw")]
        load_sp(3)
        wi_raw.append(load_weight(wi, 1, slice(0, PASS), "wi_raw"))
        load_page(1)
        load_page(2)
        list3 = load_list(offs3, "list3")
        load_page(3)
        load_wf(1)
        load_sp(4)
        load_page(4)

        put_h2(1)
        v_plane = gather(tab_plane, list1, U8, "v_plane")
        v = [gather(tab_w[c], list1, U32, "v%d" % c) for c in range(2)]
        deal_wg(wg2_turned, wg2_dealt, 2)
        deal_wg(wg2_turned, wg2_dealt, 3)
        wg1_turned = turn_wg(wg1_rows)
        wg1_dealt = keep.tile([P, PACK, S], F32, name="wg1_dealt")
        for t in range(PACK):
            deal_wg(wg1_turned, wg1_dealt, t)
        put_h2(2)
        for c in range(2):
            quantise_wi(wi_raw[c], c, 0, nc.vector.tensor_copy)
        put_h2(3)
        product_a(0, "mx")
        put_h1(0)
        put_h1(1)
        product_f(1, nc.scalar.copy)
        put_h2(4)

        list5 = load_list(offs5, "list5")
        gain_dealt = keep.tile([P, 2, PACK], F32, name="gain_dealt")
        nc.sync.dma_start(out=gain_dealt[:], in_=gain.rearrange("(g p t) -> p g t", g=2, t=PACK))
        wi_raw = [load_weight(wi, c, slice(PASS, 2 * PASS), "wi_raw") for c in range(2)]
        for k in range(5, 8):
            load_sp(k)
        wt_raw = [load_weight(wt, g, slice(0, N), "wt_raw") for g in range(2)]
        for k in range(5, 8):
            load_page(k)
        wb_raw = raw_tile([P, 2, N], I32, "wb_raw")
        nc.sync.dma_start(out=wb_raw[:], in_=wb_words.rearrange("g p n t -> p g (n t)").bitcast(I32))
        load_scales(wb_plane_raw, wb_scales)

        for c in range(2):
            quantise_wi(wi_raw[c], c, 1, nc.scalar.copy)
        for k in range(5, 8):
            put_h2(k)
        put_h1(2)
        put_h1(3)
        product_a(1, "turn")
        for k in range(4, 8):
            put_h1(k)

        z_rows0 = keep.tile([P, PACK, PJ], BF16, name="z_rows0", tag="tab_w0", align_bytes=64)
        spare = keep.tile([P, 2, PACK, CHUNK], F32, name="spare", tag="tab_w1", align_bytes=64)
        wt_q = []
        for g in range(2):
            grouped = bf_tile(N * PACK, "wt_bf")
            nc.scalar.copy(
                grouped[:].rearrange("p (t m i) -> p m i t", t=PACK, i=PACK),
                wt_raw[g][:].rearrange("p i (m t) -> p m i t", t=PACK),
            )
            wt_q.append(quantise(grouped[:], "wt%d" % g))
        wb_w = keep.tile([P, 2, N], U32, name="wb_w", tag="tab2_w", align_bytes=64)
        wb_plane = keep.tile([P, N], U8, name="wb_plane", align_bytes=64)
        nc.vector.tensor_copy(
            wb_w[:].bitcast(I32).rearrange("p g (t m) -> p g m t", t=PACK),
            wb_raw[:].rearrange("p g (m t) -> p g m t", t=PACK),
        )
        nc.vector.tensor_copy(
            wb_plane[:].rearrange("p (t m) -> p t m", t=PACK),
            wb_plane_raw[:].rearrange("p (m t) -> p t m", t=PACK),
        )
        wb_q = [(wb_w[:, g, :], wb_plane[4 * g : P, :]) for g in range(2)]

        x_of = [a_t[g][:].rearrange("p t h b m -> p t (h b m)") for g in range(2)]
        for pair in range(2):
            sines = raw_tile([P, 2, PJ], F32, "sines")
            for e in range(2):
                t = 2 * pair + e
                nc.vector.tensor_copy(x_of[0][:, t, :], pages[t][:].indirect(list5[:]))
                nc.scalar.activation(sines[:, e, :], x_of[0][:, t, :], ACT.Sin, bias=zero[:])
            for e in range(2):
                t = 2 * pair + e
                for j0 in range(0, PJ, PASS):
                    x = x_of[0][:, t, j0 : j0 + PASS]
                    sum_bank = side_bank([P, PASS], "sum_bank")
                    for jb in range(BLOCKS):
                        add_transposed(sum_bank[:, block(jb)], x[:, block(jb)], sines[:, e, j0 : j0 + PASS][:, block(jb)])
                    nc.scalar.copy(x, sum_bank[:])
                    back_bank = psum.tile([P, PASS], F32, name="back_bank", tag="turn")
                    for jb in range(BLOCKS):
                        nc.tensor.transpose(back_bank[:, block(jb)], x[:, block(jb)], ident[:])
                    nc.scalar.activation(
                        z_rows0[:, t, j0 : j0 + PASS], back_bank[:], ACT.Copy, scale=gain_dealt[:, 0, t : t + 1]
                    )
        for j0 in range(0, PJ, PASS):
            quantise_z(0, z_rows0[:, :, j0 : j0 + PASS], j0)

        y_all = keep.tile([P, PACK, PJ], F32, name="y_all", tag="half0")
        y_plane = keep.tile([P, PJ], U8, name="y_plane", align_bytes=64)
        y_rows = out_0.rearrange("(p t) j -> p t j", t=PACK)
        y_words = out_1[0].rearrange("p m t -> p (m t)").bitcast(I32)

        def product_z(bank, weight, u, j0, width):
            for e in range(2):
                for g in range(2):
                    codes, plane = weight[g]
                    nc.tensor.matmul_mx(
                        out=bank[:, e, :], lhsT=codes[:, block(2 * u + e)].bitcast(FP8X4), lhsT_scale=plane[:, block(2 * u + e)],
                        rhs=z_q[g, j0][0][:, :width].bitcast(FP8X4), rhs_scale=z_q[g, j0][1][:, :width],
                        start=(g == 0), stop=(g == 1),
                    )

        def second_stage(j0, width):
            y = y_all[:, :, j0 : j0 + width]
            for u in range(2):
                if u == 0:
                    e_bank = psum.tile([P, 2, width], F32, name="e_bank", tag="mx")
                else:
                    e_bank = side_bank([P, 2, width], "e_bank")
                b_bank = psum.tile([P, 2, width], F32, name="b_bank", tag="turn")
                product_z(e_bank, wt_q, u, j0, width)
                product_z(b_bank, wb_q, u, j0, width)
                tanh_e = small_tile([P, 2, width], F32, "tanh_e")
                nc.scalar.activation(tanh_e[:], e_bank[:], ACT.Tanh, bias=zero[:])
                nc.vector.tensor_tensor(y[:, 2 * u : 2 * u + 2, :], b_bank[:], tanh_e[:], ALU.add)
            nc.sync.dma_start(out=y_rows[:, :, j0 : j0 + width], in_=y)
            y_bf = small_tile([P, width * PACK], BF16, "y_bf")
            interleave(nc.vector.tensor_copy, y_bf[:], y)
            y_codes = keep.tile([P, width], U32, name="y_codes%d" % j0, align_bytes=64)
            nc.vector.quantize_mx(out=y_codes[:].bitcast(FP8X4), scales=y_plane[:, j0 : j0 + width], in_=y_bf[:])
            nc.sync.dma_start(out=y_words[:, j0 : j0 + width], in_=y_codes[:].bitcast(I32))

        sines_early = keep.tile([P, 2, PACK, CHUNK], F32, name="sines_early", tag="tab_w0", align_bytes=64)
        sines_late = raw_tile([P, 2, PACK, CHUNK], F32, "sines_late")
        x_cols = [x_of[1][:, :, n * CHUNK : (n + 1) * CHUNK] for n in range(PJ // CHUNK)]
        chunk_x = [x_cols[0], x_cols[1], x_cols[0], spare[:, 0, :, :]]
        chunk_sines = [sines_early[:, 0, :, :], sines_early[:, 1, :, :], sines_late[:, 0, :, :], sines_late[:, 1, :, :]]
        chunk_rows = [place.bitcast(BF16)[:, :, 0:CHUNK] for place in (spare[:, 0, :, :], spare[:, 1, :, :], x_cols[2], x_cols[3])]

        def pieces(n):
            width = P if n == PJ // CHUNK - 1 else CHUNK
            return [(j0, width) for j0 in range(n * CHUNK, (n + 1) * CHUNK, width)]

        def fetch_chunk(n):
            entries = list5[:, n * CHUNK // PER_COLUMN : (n + 1) * CHUNK // PER_COLUMN]
            for t in range(PACK):
                nc.vector.tensor_copy(chunk_x[n][:, t, :], pages[PACK + t][:].indirect(entries))

        def sine_chunk(n):
            nc.scalar.activation(chunk_sines[n], chunk_x[n], ACT.Sin, bias=zero[:])

        def make_z_chunk(n):
            nc.vector.tensor_tensor(chunk_sines[n], chunk_x[n], chunk_sines[n], ALU.add)
            for t in range(PACK):
                nc.scalar.activation(
                    chunk_rows[n][:, t, :], chunk_sines[n][:, t, :], ACT.Copy, scale=gain_dealt[:, 1, t : t + 1]
                )
            for j0, width in pieces(n):
                quantise_z(1, chunk_rows[n][:, :, j0 - n * CHUNK : j0 - n * CHUNK + width], j0)

        def finish_chunk(n):
            for j0, width in pieces(n):
                second_stage(j0, width)

        for n in range(2):
            fetch_chunk(n)
            sine_chunk(n)
        for n in range(2):
            make_z_chunk(n)
            fetch_chunk(n + 2)
        finish_chunk(0)
        sine_chunk(2)
        make_z_chunk(2)
        sine_chunk(3)
        finish_chunk(1)
        make_z_chunk(3)
        finish_chunk(2)
        finish_chunk(3)
        for q in range(QUADS):
            nc.sync.dma_start(
                out=out_2[0, 4 * q : 4 * q + 4, :].bitcast(I32), in_=y_plane[32 * q : 32 * q + 4, :].bitcast(I32)
            )
